import numpy as np
import ml_dtypes


def mxq(x, axis, fmt="e4m3"):
    dtype, down = {"e4m3": (ml_dtypes.float8_e4m3fn, 7), "e5m2": (ml_dtypes.float8_e5m2, 14)}[fmt]
    v = np.moveaxis(np.asarray(x, np.float32).astype(ml_dtypes.bfloat16).astype(np.float64), axis, -1)
    blocks = v.reshape(v.shape[:-1] + (-1, 32))
    amax = np.abs(blocks).max(-1, keepdims=True)
    byte = np.maximum(np.where(amax > 0, np.frexp(amax)[1] - 1 + 127, 0) - down, 1)
    scale = np.exp2(byte - 127.0)
    codes = (blocks / scale).astype(np.float32).astype(dtype).astype(np.float64)
    return np.moveaxis((codes * scale).reshape(v.shape), -1, axis)


WIDE = False


def mx_kscale(k):
    if not WIDE:
        return np.ones(k)
    levels = np.array([10, -10, 5, -5, 0])
    if k % 512:
        return np.exp2(np.random.permutation(np.resize(levels, k // 32))).repeat(32)
    a = np.empty((k // 512, 16))
    for p in range(k // 512):
        a[p, :8] = np.random.permutation(np.resize(levels, 8))
        for g in range(8):
            far = levels[np.abs(levels - a[p, g]) >= 10]
            a[p, g + 8] = far[np.random.randint(len(far))]
    return np.exp2(a.ravel()).repeat(32)


def f64(x):
    return np.asarray(x).astype(np.float64)


def striped8(idx):
    return np.concatenate([v.reshape(-1, 16).T for v in idx]).astype(np.uint16)


def unstriped8(offs):
    return np.stack([offs[16 * g:16 * g + 16].T.reshape(-1) for g in range(8)]).astype(np.int64)


E2M1 = np.array([0.0, 0.5, 1.0, 1.5, 2.0, 3.0, 4.0, 6.0, -0.0, -0.5, -1.0, -1.5, -2.0, -3.0, -4.0, -6.0])


def pack_weight(w, fmt):
    k, n = w.shape
    w = f64(np.asarray(w, np.float32).astype(ml_dtypes.bfloat16)).reshape(k // 32, 32, n)
    amax = np.abs(w).max(1)
    if fmt == "e4m3":
        byte = np.frexp(amax)[1] - 1 + 127 - 7
    else:
        mant, ex = np.frexp(amax / 6.0)
        byte = np.where(mant > 0.5, ex, ex - 1) + 127
    byte = np.clip(np.where(amax > 0, byte, 1), 1, 254)
    scaled = (w * np.exp2(127.0 - byte)[:, None, :]).reshape(k, n).astype(np.float32)
    by_word = np.ascontiguousarray(scaled.reshape(k // 512, 128, 4, n).transpose(0, 1, 3, 2))
    if fmt == "e4m3":
        words = by_word.astype(ml_dtypes.float8_e4m3fn).view(np.uint8)
    else:
        c = by_word.astype(ml_dtypes.float4_e2m1fn).view(np.uint8) & 0xF
        words = (c[..., 0::2] | (c[..., 1::2] << 4)).reshape(k // 512, 128, 2 * n)
    return np.ascontiguousarray(words), np.ascontiguousarray(byte.astype(np.uint8).reshape(k // 512, 16, n))


def unpack_weight(words, scales, fmt):
    g, _, n = scales.shape
    words = np.ascontiguousarray(words).reshape(g, 128, n, -1)
    if fmt == "e4m3":
        vals = words.view(ml_dtypes.float8_e4m3fn).astype(np.float64)
    else:
        nib = np.empty((g, 128, n, 4), np.uint8)
        nib[..., 0::2] = words & 0xF
        nib[..., 1::2] = words >> 4
        vals = E2M1[nib]
    vals = vals * np.repeat(np.exp2(scales.astype(np.float64) - 127.0), 8, axis=1)[..., None]
    return vals.transpose(0, 1, 3, 2).reshape(g * 512, n)


def silu(v):
    return v / (1.0 + np.exp(-np.maximum(v, -700.0)))


K, M, T, S = 1536, 1024, 1024, 512


def setup_inputs():
    n = np.random.standard_normal
    s = mx_kscale(K)[:, None]
    w = n((K, M)) / np.sqrt(K) / s
    w4 = pack_weight(w, "e2m1")
    rest = w - unpack_weight(*w4, "e2m1")
    p_r8 = pack_weight(rest, "e4m3")
    return {
        "xT": (n((K, T)) * s).astype(np.float32),
        "w4_words": w4[0],
        "w4_scales": w4[1],
        "r8_words": p_r8[0],
        "r8_scales": p_r8[1],
        "wgt": np.repeat(np.random.uniform(0.5, 2.0, (8, S)), 16, axis=0).astype(np.float32),
        "b": (0.3 * n(1024)).astype(np.float32),
        "wgo": np.repeat(np.random.uniform(0.5, 2.0, (8, S)), 16, axis=0).astype(np.float32),
        "offs": striped8(np.stack([np.random.permutation(T)[:S] for _ in range(8)])),
        "offs2": striped8(np.stack([np.random.permutation(T)[:S] for _ in range(8)])),
    }


def reference(xT, w4_words, w4_scales, r8_words, r8_scales, wgt, b, wgo, offs, offs2):
    idx = unstriped8(offs)
    group = np.arange(K) % 512 // 64
    xg = f64(wgt)[np.arange(K) // 4 % 128] * f64(xT)[np.arange(K)[:, None], idx[group]]
    xT_ = mxq(xg, 0, "e4m3")
    w4_ = unpack_weight(w4_words, w4_scales, "e2m1")
    r8_ = unpack_weight(r8_words, r8_scales, "e4m3")
    y = w4_.T @ xT_ + r8_.T @ xT_
    place = unstriped8(offs2)[np.arange(M) % 128 // 16]
    out = np.zeros((M, T))
    out[np.arange(M)[:, None], place] = f64(wgo)[np.arange(M) % 128] * (silu(y + f64(b)[:, None]))
    return out

@@ -1,0 +1,224 @@
+from contextlib import ExitStack
+
+import concourse.mybir as mybir
+from concourse.masks import make_identity
+
+F32 = mybir.dt.float32
+BF16 = mybir.dt.bfloat16
+I32 = mybir.dt.int32
+U32 = mybir.dt.uint32
+U16 = mybir.dt.uint16
+U8 = mybir.dt.uint8
+FP8X4 = mybir.dt.float8_e4m3fn_x4
+FP4X4 = mybir.dt.float4_e2m1fn_x4
+MULT = mybir.AluOpType.mult
+SILU = mybir.ActivationFunctionType.Silu
+
+K, M, T, S = 1536, 1024, 1024, 512
+P = 128
+PACK = 4
+PASSES = K // (P * PACK)
+ROWS = M // P
+HALF = S // 2
+QUARTER = S // 4
+HALF_COLS = HALF // 16
+WINDOWS = 4
+FLOPS = 2 * 2 * K * M * S
+
+
+def tile_list_hboth_silu_kernel(
+    tc, xT, w4_words, w4_scales, r8_words, r8_scales, wgt, b, wgo, offs, offs2, out
+):
+    nc = tc.nc
+    with ExitStack() as ctx:
+        held = ctx.enter_context(tc.tile_pool(name="held", bufs=1))
+        psum = ctx.enter_context(tc.psum_pool(name="psum", bufs=1))
+
+        offs_t = held.tile([P, S // 16], U16, name="offs_t")
+        offs2_t = held.tile([P, S // 16], U16, name="offs2_t")
+        wgt_t = [held.tile([P, HALF], F32, name=f"wgt{h}") for h in range(2)]
+        wgo_t = [held.tile([P, HALF], F32, name=f"wgo{h}") for h in range(2)]
+        planes = [[held.tile([P, T], F32, name=f"x{a}_{i}") for i in range(PACK)] for a in range(PASSES)]
+        picked = [held.tile([P, PACK, S], F32, name=f"picked{a}") for a in range(PASSES)]
+        grouped = [held.tile([P, S, PACK], BF16, name=f"grouped{a}", align_bytes=64) for a in range(PASSES)]
+        codes = [held.tile([P, S], U32, name=f"codes{a}", align_bytes=64) for a in range(PASSES)]
+        scales = [held.tile([P, S], U8, name=f"scales{a}", align_bytes=64) for a in range(PASSES)]
+        w4_t = held.tile([P, PASSES, 2 * M], U8, name="w4_t", align_bytes=64)
+        r8_t = held.tile([P, PASSES, 4 * M], U8, name="r8_t", align_bytes=64)
+        w_s = held.tile([P, PASSES, M], U8, name="w_s", align_bytes=64)
+        windows = [held.tile([P, T], F32, name=f"window{w}") for w in range(WINDOWS)]
+        acts = [held.tile([P, S], F32, name=f"act{r}") for r in range(ROWS)]
+        b_rows = held.tile([P, P], F32, name="b_rows")
+        ident = held.tile([P, P], F32, name="ident")
+        bias = held.tile([P, ROWS], F32, name="bias")
+        dummy = held.tile([P, 2], F32, name="dummy")
+        banks = [psum.tile([P, 512], F32, name=f"bank{k}") for k in range(8)]
+
+        x_rows = xT.rearrange("(a p i) t -> a i p t", p=P, i=PACK)
+        w4_src = w4_words.bitcast(I32).rearrange("a p c -> p a c")
+        r8_src = r8_words.rearrange("a p n i -> a p (n i)").bitcast(I32).rearrange("a p c -> p a c")
+
+        nc.gpsimd.memset(dummy[:], 0.0)
+        nc.gpsimd.memset(w_s[:].bitcast(I32), 0)
+        nc.gpsimd.memset(b_rows[:], 0.0)
+        make_identity(nc, ident[:])
+        for w in range(WINDOWS):
+            nc.vector.memset(windows[w][:], 0.0)
+        nc.scalar.activation(dummy[:, 1:2], dummy[:, 0:1], SILU)
+
+        for q in range(4):
+            for first, src in ((0, w4_scales), (4, r8_scales)):
+                nc.scalar.dma_start(
+                    w_s[32 * q + first : 32 * q + first + 4].bitcast(I32),
+                    src[:, 4 * q : 4 * q + 4, :].bitcast(I32).rearrange("a r n -> r a n"),
+                )
+
+        nc.sync.dma_start(offs_t[:], offs)
+        nc.sync.dma_start(wgt_t[0][:], wgt[:, 0:HALF])
+        nc.sync.dma_start(planes[0][0][:], x_rows[0, 0])
+        nc.sync.dma_start(wgt_t[1][:], wgt[:, HALF:S])
+        for i in range(1, PACK):
+            nc.sync.dma_start(planes[0][i][:], x_rows[0, i])
+        nc.sync.dma_start(offs2_t[:], offs2)
+        nc.sync.dma_start(b_rows[0:ROWS, :], b.rearrange("(r p) -> r p", p=P))
+        for a in range(1, PASSES):
+            for i in range(PACK):
+                nc.sync.dma_start(planes[a][i][:], x_rows[a, i])
+
+        def load_weights(h):
+            c4 = slice(h * M // 8, (h + 1) * M // 8)
+            c8 = slice(h * M // 4, (h + 1) * M // 4)
+            nc.sync.dma_start(w4_t[:].bitcast(I32)[:, :, c4], w4_src[:, :, c4])
+            nc.sync.dma_start(r8_t[:].bitcast(I32)[:, :, c8], r8_src[:, :, c8])
+
+        load_weights(0)
+        for h in range(2):
+            nc.sync.dma_start(wgo_t[h][:], wgo[:, h * HALF : (h + 1) * HALF])
+            load_weights(1 + h)
+        load_weights(3)
+
+        nc.tensor.transpose(banks[7][:, 0:P], b_rows[:], ident[:])
+        nc.scalar.copy(bias[:], banks[7][:, 0:ROWS])
+
+        def gather(a, i, h):
+            nc.vector.tensor_tensor(
+                picked[a][:, i, h * HALF : (h + 1) * HALF],
+                planes[a][i][:].indirect(offs_t[:, h * HALF_COLS : (h + 1) * HALF_COLS]),
+                wgt_t[h][:],
+                MULT,
+            )
+
+        def interleaved(a, c0, c1):
+            return (
+                grouped[a][:, c0:c1, :].rearrange("p (c j) i -> p c i j", j=4),
+                picked[a][:, :, c0:c1].rearrange("p i (c j) -> p c i j", j=4),
+            )
+
+        def interleave(a, c0, c1):
+            nc.scalar.copy(*interleaved(a, c0, c1))
+
+        def quantize(a, c0, c1):
+            nc.vector.quantize_mx(
+                out=codes[a][:, c0:c1].bitcast(FP8X4),
+                scales=scales[a][:, c0:c1],
+                in_=grouped[a][:, c0:c1, :].rearrange("p c i -> p (c i)"),
+            )
+
+        def multiply(dst, r, a, c0, c1):
+            for kind in range(2):
+                if kind == 0:
+                    lhsT = w4_t[:, a, 2 * P * r : 2 * P * (r + 1)].bitcast(FP4X4)
+                    lhsT_scale = w_s[:, a, P * r : P * (r + 1)]
+                else:
+                    lhsT = r8_t[:, a, 4 * P * r : 4 * P * (r + 1)].bitcast(FP8X4)
+                    lhsT_scale = w_s[4:P, a, P * r : P * (r + 1)]
+                nc.tensor.matmul_mx(
+                    out=dst,
+                    lhsT=lhsT,
+                    lhsT_scale=lhsT_scale,
+                    rhs=codes[a][:, c0:c1].bitcast(FP8X4),
+                    rhs_scale=scales[a][:, c0:c1],
+                    start=(a == 0 and kind == 0),
+                    stop=(a == PASSES - 1 and kind == 1),
+                )
+
+        last = PASSES - 1
+        open_a = [(0, 0, 0), (1, 0, 1)]
+        open_b = [(4, 0, 2), (5, 0, 3)]
+
+        def multiply_open(groups, a):
+            for k, r, q in groups:
+                multiply(banks[k][:, 0:QUARTER], r, a, q * QUARTER, (q + 1) * QUARTER)
+
+        LAG = 4
+        for n in range(PASSES * PACK):
+            a, i = n // PACK, n % PACK
+            gather(a, i, 0)
+            if n == 2 * PACK:
+                quantize(0, 0, S)
+                multiply_open(open_a, 0)
+            if n == 2 * PACK + 2:
+                quantize(1, 0, HALF)
+                multiply_open(open_a, 1)
+            if i == PACK - 1:
+                interleave(a, 0, QUARTER if a == last else HALF)
+            if n >= LAG:
+                a, i = (n - LAG) // PACK, (n - LAG) % PACK
+                gather(a, i, 1)
+                if i == PACK - 1:
+                    interleave(a, HALF, S)
+        nc.vector.tensor_copy(*interleaved(last, QUARTER, HALF))
+        for i in range(PACK):
+            gather(last, i, 1)
+            if i == 0:
+                quantize(last, 0, HALF)
+                multiply_open(open_a, last)
+        interleave(last, HALF, S)
+        quantize(1, HALF, S)
+        for a in range(last):
+            multiply_open(open_b, a)
+
+        def activate(r, c0, src):
+            c1 = c0 + src.shape[1]
+            nc.scalar.activation(acts[r][:, c0:c1], src, SILU, bias=bias[:, r : r + 1])
+
+        def scatter(r, h):
+            cols = slice(h * HALF, (h + 1) * HALF)
+            nc.vector.tensor_tensor(
+                windows[r % WINDOWS][:].indirect(offs2_t[:, h * HALF_COLS : (h + 1) * HALF_COLS]),
+                acts[r][:, cols],
+                wgo_t[h][:],
+                MULT,
+            )
+            if h == 1:
+                nc.sync.dma_start(out[P * r : P * (r + 1), :], windows[r % WINDOWS][:])
+
+        def late(r, dst, c0, c1):
+            for a in range(PASSES):
+                multiply(dst, r, a, c0, c1)
+
+        for k in range(2):
+            activate(0, k * QUARTER, banks[k][:, 0:QUARTER])
+        scatter(0, 0)
+        for k in range(2):
+            late(1, banks[2][:, k * QUARTER : (k + 1) * QUARTER], k * QUARTER, (k + 1) * QUARTER)
+        activate(1, 0, banks[2][:, 0:HALF])
+        quantize(last, HALF, S)
+        multiply_open(open_b, last)
+        for k in range(2):
+            activate(0, HALF + k * QUARTER, banks[4 + k][:, 0:QUARTER])
+        scatter(1, 0)
+        scatter(0, 1)
+        for k in range(2):
+            late(1, banks[6][:, k * QUARTER : (k + 1) * QUARTER], HALF + k * QUARTER, HALF + (k + 1) * QUARTER)
+        activate(1, HALF, banks[6][:, 0:HALF])
+        scatter(1, 1)
+        bank_of = (7, 0, 1, 2, 3, 4)
+        for r0 in range(2, ROWS, 2):
+            for r in (r0, r0 + 1):
+                bank = banks[bank_of[r - 2]]
+                late(r, bank[:], 0, S)
+                activate(r, 0, bank[:])
+            for h in range(2):
+                for r in (r0, r0 + 1):
+                    scatter(r, h)

@@ -22,7 +22,8 @@ ROWS = M // P
 HALF = S // 2
 QUARTER = S // 4
 HALF_COLS = HALF // 16
-WINDOWS = 4
+WINDOWS = 3
+EARLY = 2 * P
 FLOPS = 2 * 2 * K * M * S
 
 
@@ -30,22 +31,43 @@ def tile_list_hboth_silu_kernel(
     tc, xT, w4_words, w4_scales, r8_words, r8_scales, wgt, b, wgo, offs, offs2, out
 ):
     nc = tc.nc
+    last = PASSES - 1
     with ExitStack() as ctx:
         held = ctx.enter_context(tc.tile_pool(name="held", bufs=1))
         psum = ctx.enter_context(tc.psum_pool(name="psum", bufs=1))
 
         offs_t = held.tile([P, S // 16], U16, name="offs_t")
         offs2_t = held.tile([P, S // 16], U16, name="offs2_t")
-        wgt_t = [held.tile([P, HALF], F32, name=f"wgt{h}") for h in range(2)]
-        wgo_t = [held.tile([P, HALF], F32, name=f"wgo{h}") for h in range(2)]
-        planes = [[held.tile([P, T], F32, name=f"x{a}_{i}") for i in range(PACK)] for a in range(PASSES)]
-        picked = [held.tile([P, PACK, S], F32, name=f"picked{a}") for a in range(PASSES)]
-        grouped = [held.tile([P, S, PACK], BF16, name=f"grouped{a}", align_bytes=64) for a in range(PASSES)]
-        codes = [held.tile([P, S], U32, name=f"codes{a}", align_bytes=64) for a in range(PASSES)]
+        shared = held.tile([P, 6 * HALF], F32, name="shared")
+        wgt1 = held.tile([P, HALF], F32, name="wgt1")
+        wgt_t = [shared[:, QUARTER : QUARTER + HALF], wgt1[:]]
+        wgo_t = held.tile([P, S], F32, name="wgo_t")
+        planes = [
+            [held.tile([P, T], F32, name=f"x{a}_{i}", tag=f"x{a}_{i}", align_bytes=64) for i in range(PACK)]
+            for a in range(PASSES)
+        ]
+        picked = {}
+        grouped = {}
+        for a in range(PASSES):
+            if a < last:
+                g = held.tile([P, S * PACK], BF16, name=f"grouped{a}", align_bytes=64)
+                for h in range(2):
+                    picked[a, h] = held.tile([P, PACK * HALF], F32, name=f"picked{a}_{h}")[:]
+                    grouped[a, h] = g[:, h * HALF * PACK : (h + 1) * HALF * PACK]
+                grouped[a] = g[:]
+        picked[last, 0] = shared[:, 2 * HALF : 6 * HALF]
+        picked[last, 1] = shared[:, 0 : 4 * HALF]
+        for h in range(2):
+            grouped[last, h] = held.tile([P, HALF * PACK], BF16, name=f"grouped_last{h}", align_bytes=64)[:]
+        codes = {a: held.tile([P, S], U32, name=f"codes{a}", align_bytes=64) for a in range(1, PASSES)}
         scales = [held.tile([P, S], U8, name=f"scales{a}", align_bytes=64) for a in range(PASSES)]
-        w4_t = held.tile([P, PASSES, 2 * M], U8, name="w4_t", align_bytes=64)
-        r8_t = held.tile([P, PASSES, 4 * M], U8, name="r8_t", align_bytes=64)
-        w_s = held.tile([P, PASSES, M], U8, name="w_s", align_bytes=64)
+        chunks = ((0, EARLY), (EARLY, 2 * EARLY), (2 * EARLY, M))
+        w4_t = {c0: held.tile([P, PASSES, 2 * (c1 - c0)], U8, name=f"w4_{c0}", align_bytes=64) for c0, c1 in chunks}
+        r8_t = {c0: held.tile([P, PASSES, 4 * (c1 - c0)], U8, name=f"r8_{c0}", align_bytes=64) for c0, c1 in chunks}
+        w_s = {
+            0: held.tile([P, PASSES, EARLY], U8, name="scales_early", align_bytes=64),
+            EARLY: held.tile([P, PASSES, M - EARLY], U8, name="scales_late", align_bytes=64),
+        }
         windows = [held.tile([P, T], F32, name=f"window{w}") for w in range(WINDOWS)]
         acts = [held.tile([P, S], F32, name=f"act{r}") for r in range(ROWS)]
         b_rows = held.tile([P, P], F32, name="b_rows")
@@ -59,24 +81,33 @@ def tile_list_hboth_silu_kernel(
         r8_src = r8_words.rearrange("a p n i -> a p (n i)").bitcast(I32).rearrange("a p c -> p a c")
 
         nc.gpsimd.memset(dummy[:], 0.0)
-        nc.gpsimd.memset(w_s[:].bitcast(I32), 0)
+        nc.vector.memset(w_s[0][:].bitcast(I32), 0)
         nc.gpsimd.memset(b_rows[:], 0.0)
         make_identity(nc, ident[:])
-        for w in range(WINDOWS):
+        nc.gpsimd.memset(w_s[EARLY][:].bitcast(I32), 0)
+        nc.gpsimd.memset(windows[2][:], 0.0)
+        for w in range(2):
             nc.vector.memset(windows[w][:], 0.0)
         nc.scalar.activation(dummy[:, 1:2], dummy[:, 0:1], SILU)
 
-        for q in range(4):
-            for first, src in ((0, w4_scales), (4, r8_scales)):
-                nc.scalar.dma_start(
-                    w_s[32 * q + first : 32 * q + first + 4].bitcast(I32),
-                    src[:, 4 * q : 4 * q + 4, :].bitcast(I32).rearrange("a r n -> r a n"),
-                )
+        def load_scales(queue, c0, c1):
+            for q in range(4):
+                for first, src in ((0, w4_scales), (4, r8_scales)):
+                    queue.dma_start(
+                        w_s[c0][32 * q + first : 32 * q + first + 4].bitcast(I32),
+                        src[:, 4 * q : 4 * q + 4, c0:c1].bitcast(I32).rearrange("a r n -> r a n"),
+                    )
 
+        def load_weights(c0, c1):
+            c4 = slice(c0 // 2, c1 // 2)
+            nc.sync.dma_start(w4_t[c0][:].bitcast(I32), w4_src[:, :, c4])
+            nc.sync.dma_start(r8_t[c0][:].bitcast(I32), r8_src[:, :, c0:c1])
+
+        load_scales(nc.scalar, 0, EARLY)
         nc.sync.dma_start(offs_t[:], offs)
-        nc.sync.dma_start(wgt_t[0][:], wgt[:, 0:HALF])
+        nc.sync.dma_start(wgt_t[0], wgt[:, 0:HALF])
         nc.sync.dma_start(planes[0][0][:], x_rows[0, 0])
-        nc.sync.dma_start(wgt_t[1][:], wgt[:, HALF:S])
+        nc.sync.dma_start(wgt_t[1], wgt[:, HALF:S])
         for i in range(1, PACK):
             nc.sync.dma_start(planes[0][i][:], x_rows[0, i])
         nc.sync.dma_start(offs2_t[:], offs2)
@@ -84,54 +115,47 @@ def tile_list_hboth_silu_kernel(
         for a in range(1, PASSES):
             for i in range(PACK):
                 nc.sync.dma_start(planes[a][i][:], x_rows[a, i])
-
-        def load_weights(h):
-            c4 = slice(h * M // 8, (h + 1) * M // 8)
-            c8 = slice(h * M // 4, (h + 1) * M // 4)
-            nc.sync.dma_start(w4_t[:].bitcast(I32)[:, :, c4], w4_src[:, :, c4])
-            nc.sync.dma_start(r8_t[:].bitcast(I32)[:, :, c8], r8_src[:, :, c8])
-
-        load_weights(0)
-        for h in range(2):
-            nc.sync.dma_start(wgo_t[h][:], wgo[:, h * HALF : (h + 1) * HALF])
-            load_weights(1 + h)
-        load_weights(3)
+        load_weights(0, EARLY)
+        nc.sync.dma_start(wgo_t[:, 0:HALF], wgo[:, 0:HALF])
+        load_scales(nc.sync, EARLY, M)
+        load_weights(EARLY, 2 * EARLY)
+        nc.sync.dma_start(wgo_t[:, HALF:S], wgo[:, HALF:S])
+        load_weights(2 * EARLY, M)
 
         nc.tensor.transpose(banks[7][:, 0:P], b_rows[:], ident[:])
         nc.scalar.copy(bias[:], banks[7][:, 0:ROWS])
+        first_bias = grouped[last, 1][:, 0:2].bitcast(F32)
+        nc.scalar.copy(first_bias, banks[7][:, 0:1])
 
         def gather(a, i, h):
             nc.vector.tensor_tensor(
-                picked[a][:, i, h * HALF : (h + 1) * HALF],
+                picked[a, h][:, i * HALF : (i + 1) * HALF],
                 planes[a][i][:].indirect(offs_t[:, h * HALF_COLS : (h + 1) * HALF_COLS]),
-                wgt_t[h][:],
+                wgt_t[h],
                 MULT,
             )
 
-        def interleaved(a, c0, c1):
-            return (
-                grouped[a][:, c0:c1, :].rearrange("p (c j) i -> p c i j", j=4),
-                picked[a][:, :, c0:c1].rearrange("p i (c j) -> p c i j", j=4),
+        def interleave(a, h):
+            nc.scalar.copy(
+                grouped[a, h].rearrange("p (c j i) -> p c i j", j=4, i=PACK),
+                picked[a, h].rearrange("p (i c j) -> p c i j", j=4, i=PACK),
             )
 
-        def interleave(a, c0, c1):
-            nc.scalar.copy(*interleaved(a, c0, c1))
-
-        def quantize(a, c0, c1):
-            nc.vector.quantize_mx(
-                out=codes[a][:, c0:c1].bitcast(FP8X4),
-                scales=scales[a][:, c0:c1],
-                in_=grouped[a][:, c0:c1, :].rearrange("p c i -> p (c i)"),
-            )
+        def quantize(a, c0, c1, src):
+            nc.vector.quantize_mx(out=codes[a][:, c0:c1].bitcast(FP8X4), scales=scales[a][:, c0:c1], in_=src)
 
         def multiply(dst, r, a, c0, c1):
+            base = 0 if P * r < EARLY else EARLY
+            cols = slice(P * r - base, P * (r + 1) - base)
+            chunk = max(c0 for c0, c1 in chunks if c0 <= P * r)
+            n0 = P * r - chunk
             for kind in range(2):
                 if kind == 0:
-                    lhsT = w4_t[:, a, 2 * P * r : 2 * P * (r + 1)].bitcast(FP4X4)
-                    lhsT_scale = w_s[:, a, P * r : P * (r + 1)]
+                    lhsT = w4_t[chunk][:, a, 2 * n0 : 2 * (n0 + P)].bitcast(FP4X4)
+                    lhsT_scale = w_s[base][:, a, cols]
                 else:
-                    lhsT = r8_t[:, a, 4 * P * r : 4 * P * (r + 1)].bitcast(FP8X4)
-                    lhsT_scale = w_s[4:P, a, P * r : P * (r + 1)]
+                    lhsT = r8_t[chunk][:, a, 4 * n0 : 4 * (n0 + P)].bitcast(FP8X4)
+                    lhsT_scale = w_s[base][4:P, a, cols]
                 nc.tensor.matmul_mx(
                     out=dst,
                     lhsT=lhsT,
@@ -139,86 +163,80 @@ def tile_list_hboth_silu_kernel(
                     rhs=codes[a][:, c0:c1].bitcast(FP8X4),
                     rhs_scale=scales[a][:, c0:c1],
                     start=(a == 0 and kind == 0),
-                    stop=(a == PASSES - 1 and kind == 1),
+                    stop=(a == last and kind == 1),
                 )
 
-        last = PASSES - 1
-        open_a = [(0, 0, 0), (1, 0, 1)]
-        open_b = [(4, 0, 2), (5, 0, 3)]
-
-        def multiply_open(groups, a):
-            for k, r, q in groups:
-                multiply(banks[k][:, 0:QUARTER], r, a, q * QUARTER, (q + 1) * QUARTER)
-
-        LAG = 4
-        for n in range(PASSES * PACK):
-            a, i = n // PACK, n % PACK
-            gather(a, i, 0)
-            if n == 2 * PACK:
-                quantize(0, 0, S)
-                multiply_open(open_a, 0)
-            if n == 2 * PACK + 2:
-                quantize(1, 0, HALF)
-                multiply_open(open_a, 1)
-            if i == PACK - 1:
-                interleave(a, 0, QUARTER if a == last else HALF)
-            if n >= LAG:
-                a, i = (n - LAG) // PACK, (n - LAG) % PACK
-                gather(a, i, 1)
-                if i == PACK - 1:
-                    interleave(a, HALF, S)
-        nc.vector.tensor_copy(*interleaved(last, QUARTER, HALF))
-        for i in range(PACK):
-            gather(last, i, 1)
-            if i == 0:
-                quantize(last, 0, HALF)
-                multiply_open(open_a, last)
-        interleave(last, HALF, S)
-        quantize(1, HALF, S)
-        for a in range(last):
-            multiply_open(open_b, a)
+        def multiply_open(h, a):
+            for q in (2 * h, 2 * h + 1):
+                multiply(banks[q][:, 0:QUARTER], 0, a, q * QUARTER, (q + 1) * QUARTER)
 
         def activate(r, c0, src):
             c1 = c0 + src.shape[1]
-            nc.scalar.activation(acts[r][:, c0:c1], src, SILU, bias=bias[:, r : r + 1])
+            column = first_bias if r == 0 and c1 <= HALF else bias[:, r : r + 1]
+            nc.scalar.activation(acts[r][:, c0:c1], src, SILU, bias=column)
 
-        def scatter(r, h):
+        def store(r):
+            nc.sync.dma_start(out[P * r : P * (r + 1), :], windows[r % WINDOWS][:])
+
+        def scatter_half(r, h):
             cols = slice(h * HALF, (h + 1) * HALF)
             nc.vector.tensor_tensor(
                 windows[r % WINDOWS][:].indirect(offs2_t[:, h * HALF_COLS : (h + 1) * HALF_COLS]),
                 acts[r][:, cols],
-                wgo_t[h][:],
+                wgo_t[:, cols],
                 MULT,
             )
-            if h == 1:
-                nc.sync.dma_start(out[P * r : P * (r + 1), :], windows[r % WINDOWS][:])
 
         def late(r, dst, c0, c1):
             for a in range(PASSES):
                 multiply(dst, r, a, c0, c1)
 
-        for k in range(2):
-            activate(0, k * QUARTER, banks[k][:, 0:QUARTER])
-        scatter(0, 0)
-        for k in range(2):
-            late(1, banks[2][:, k * QUARTER : (k + 1) * QUARTER], k * QUARTER, (k + 1) * QUARTER)
-        activate(1, 0, banks[2][:, 0:HALF])
-        quantize(last, HALF, S)
-        multiply_open(open_b, last)
-        for k in range(2):
-            activate(0, HALF + k * QUARTER, banks[4 + k][:, 0:QUARTER])
-        scatter(1, 0)
-        scatter(0, 1)
-        for k in range(2):
-            late(1, banks[6][:, k * QUARTER : (k + 1) * QUARTER], HALF + k * QUARTER, HALF + (k + 1) * QUARTER)
-        activate(1, HALF, banks[6][:, 0:HALF])
-        scatter(1, 1)
-        bank_of = (7, 0, 1, 2, 3, 4)
-        for r0 in range(2, ROWS, 2):
-            for r in (r0, r0 + 1):
-                bank = banks[bank_of[r - 2]]
-                late(r, bank[:], 0, S)
-                activate(r, 0, bank[:])
-            for h in range(2):
-                for r in (r0, r0 + 1):
-                    scatter(r, h)
+        def late_half(r, h, bank):
+            for k in range(2):
+                late(r, bank[:, k * QUARTER : (k + 1) * QUARTER], h * HALF + k * QUARTER, h * HALF + (k + 1) * QUARTER)
+            activate(r, h * HALF, bank[:, 0:HALF])
+
+        for a in range(last):
+            for i in range(PACK):
+                for h in range(2):
+                    gather(a, i, h)
+                    if i == PACK - 1:
+                        interleave(a, h)
+        for i in range(PACK):
+            gather(last, i, 0)
+        interleave(last, 0)
+        codes[0] = held.tile([P, S], U32, name="codes0", tag="x1_1", align_bytes=64)
+        quantize(0, 0, S, grouped[0])
+        for h in range(2):
+            quantize(1, h * HALF, (h + 1) * HALF, grouped[1, h])
+        for a in range(last):
+            multiply_open(0, a)
+        for i in range(2):
+            gather(last, i, 1)
+        quantize(last, 0, HALF, grouped[last, 0])
+        multiply_open(0, last)
+        for i in range(2, PACK):
+            gather(last, i, 1)
+        for q in range(2):
+            activate(0, q * QUARTER, banks[q][:, 0:QUARTER])
+        interleave(last, 1)
+        scatter_half(0, 0)
+        late_half(1, 0, banks[4])
+        for a in range(last):
+            multiply_open(1, a)
+        quantize(last, HALF, S, grouped[last, 1])
+        multiply_open(1, last)
+        for q in range(2, 4):
+            activate(0, q * QUARTER, banks[q][:, 0:QUARTER])
+        scatter_half(1, 0)
+        scatter_half(0, 1)
+        store(0)
+        late_half(1, 1, banks[5])
+        scatter_half(1, 1)
+        store(1)
+        for r in range(2, ROWS):
+            bank = banks[(0, 1, 4, 2, 3, 5)[r - 2]]
+            late(r, bank[:], 0, S)
+            activate(r, 0, bank[:])
+            nc.vector.tensor_tensor(windows[r % WINDOWS][:].indirect(offs2_t[:]), acts[r][:], wgo_t[:], MULT)
+            store(r)

@@ -18,12 +18,16 @@ K, M, T, S = 1536, 1024, 1024, 512
 P = 128
 PACK = 4
 PASSES = K // (P * PACK)
+PLANES = PASSES * PACK
 ROWS = M // P
 HALF = S // 2
 QUARTER = S // 4
-HALF_COLS = HALF // 16
 WINDOWS = 3
 EARLY = 2 * P
+CHUNKS = ((0, P), (P, 2 * P), (2 * P, 4 * P), (4 * P, M))
+FRONT, REST, WHOLE = (0, HALF), (HALF, S), (0, S)
+BIAS_PIECES = ((0, 2), (2, 4), (4, 8))
+BIAS_BEHIND = (6, 10, 11)
 FLOPS = 2 * 2 * K * M * S
 
 
@@ -38,41 +42,34 @@ def tile_list_hboth_silu_kernel(
 
         offs_t = held.tile([P, S // 16], U16, name="offs_t")
         offs2_t = held.tile([P, S // 16], U16, name="offs2_t")
-        shared = held.tile([P, 6 * HALF], F32, name="shared")
-        wgt1 = held.tile([P, HALF], F32, name="wgt1")
-        wgt_t = [shared[:, QUARTER : QUARTER + HALF], wgt1[:]]
+        wgt_t = held.tile([P, S], F32, name="wgt_t")
         wgo_t = held.tile([P, S], F32, name="wgo_t")
-        planes = [
-            [held.tile([P, T], F32, name=f"x{a}_{i}", tag=f"x{a}_{i}", align_bytes=64) for i in range(PACK)]
-            for a in range(PASSES)
+        planes = [held.tile([P, T], F32, name=f"x{n}", tag=f"x{n}", align_bytes=64) for n in range(PLANES)]
+        picked = [
+            held.tile([P, PACK * S], F32, name=f"picked{a}")[:].rearrange("p (i s) -> p i s", i=PACK) for a in range(last)
         ]
-        picked = {}
-        grouped = {}
-        for a in range(PASSES):
-            if a < last:
-                g = held.tile([P, S * PACK], BF16, name=f"grouped{a}", align_bytes=64)
-                for h in range(2):
-                    picked[a, h] = held.tile([P, PACK * HALF], F32, name=f"picked{a}_{h}")[:]
-                    grouped[a, h] = g[:, h * HALF * PACK : (h + 1) * HALF * PACK]
-                grouped[a] = g[:]
-        picked[last, 0] = shared[:, 2 * HALF : 6 * HALF]
-        picked[last, 1] = shared[:, 0 : 4 * HALF]
-        for h in range(2):
-            grouped[last, h] = held.tile([P, HALF * PACK], BF16, name=f"grouped_last{h}", align_bytes=64)[:]
-        codes = {a: held.tile([P, S], U32, name=f"codes{a}", align_bytes=64) for a in range(1, PASSES)}
+        grouped = [held.tile([P, S * PACK], BF16, name=f"grouped{a}", align_bytes=64) for a in range(last)]
+        shared = held.tile([P, 6 * HALF], F32, name="shared")
+        picked_front = shared[:, 2 * HALF : 6 * HALF].rearrange("p (i s) -> p i s", i=PACK)
+        picked_rest = shared[:, 0 : 4 * HALF].rearrange("p (i s) -> p i s", i=PACK)
+        grouped_last = {
+            part: held.tile([P, HALF * PACK], BF16, name=f"grouped_last{part[0]}", align_bytes=64) for part in (FRONT, REST)
+        }
+        codes = {last: held.tile([P, S], U32, name="codes_last", align_bytes=64)}
         scales = [held.tile([P, S], U8, name=f"scales{a}", align_bytes=64) for a in range(PASSES)]
-        chunks = ((0, EARLY), (EARLY, 2 * EARLY), (2 * EARLY, M))
-        w4_t = {c0: held.tile([P, PASSES, 2 * (c1 - c0)], U8, name=f"w4_{c0}", align_bytes=64) for c0, c1 in chunks}
-        r8_t = {c0: held.tile([P, PASSES, 4 * (c1 - c0)], U8, name=f"r8_{c0}", align_bytes=64) for c0, c1 in chunks}
+        w4_t = {c0: held.tile([P, PASSES, 2 * (c1 - c0)], U8, name=f"w4_{c0}", align_bytes=64) for c0, c1 in CHUNKS}
+        r8_t = {c0: held.tile([P, PASSES, 4 * (c1 - c0)], U8, name=f"r8_{c0}", align_bytes=64) for c0, c1 in CHUNKS}
         w_s = {
             0: held.tile([P, PASSES, EARLY], U8, name="scales_early", align_bytes=64),
             EARLY: held.tile([P, PASSES, M - EARLY], U8, name="scales_late", align_bytes=64),
         }
         windows = [held.tile([P, T], F32, name=f"window{w}") for w in range(WINDOWS)]
         acts = [held.tile([P, S], F32, name=f"act{r}") for r in range(ROWS)]
-        b_rows = held.tile([P, P], F32, name="b_rows")
+        b_rows = [held.tile([P, P], F32, name=f"b_rows{k}", tag=f"b_rows{k}", align_bytes=64)[:] for k in range(2)]
+        b_rows.append(shared[:, HALF - P // 2 : HALF + P // 2])
         ident = held.tile([P, P], F32, name="ident")
         bias = held.tile([P, ROWS], F32, name="bias")
+        first_bias = grouped_last[REST][:, 0:2].bitcast(F32)
         dummy = held.tile([P, 2], F32, name="dummy")
         banks = [psum.tile([P, 512], F32, name=f"bank{k}") for k in range(8)]
 
@@ -82,161 +79,168 @@ def tile_list_hboth_silu_kernel(
 
         nc.gpsimd.memset(dummy[:], 0.0)
         nc.vector.memset(w_s[0][:].bitcast(I32), 0)
-        nc.gpsimd.memset(b_rows[:], 0.0)
+        nc.vector.memset(windows[0][:], 0.0)
+        for rows in b_rows:
+            nc.gpsimd.memset(rows, 0.0)
         make_identity(nc, ident[:])
         nc.gpsimd.memset(w_s[EARLY][:].bitcast(I32), 0)
-        nc.gpsimd.memset(windows[2][:], 0.0)
-        for w in range(2):
-            nc.vector.memset(windows[w][:], 0.0)
+        for w in range(1, WINDOWS):
+            nc.gpsimd.memset(windows[w][:], 0.0)
         nc.scalar.activation(dummy[:, 1:2], dummy[:, 0:1], SILU)
 
-        def load_scales(queue, c0, c1):
-            for q in range(4):
-                for first, src in ((0, w4_scales), (4, r8_scales)):
-                    queue.dma_start(
-                        w_s[c0][32 * q + first : 32 * q + first + 4].bitcast(I32),
-                        src[:, 4 * q : 4 * q + 4, c0:c1].bitcast(I32).rearrange("a r n -> r a n"),
-                    )
+        def load_scales(piece, c0, c1):
+            q, kind = divmod(piece, 2)
+            first, src = ((0, w4_scales), (4, r8_scales))[kind]
+            nc.sync.dma_start(
+                w_s[c0][32 * q + first : 32 * q + first + 4].bitcast(I32),
+                src[:, 4 * q : 4 * q + 4, c0:c1].bitcast(I32).rearrange("a r n -> r a n"),
+            )
 
         def load_weights(c0, c1):
-            c4 = slice(c0 // 2, c1 // 2)
-            nc.sync.dma_start(w4_t[c0][:].bitcast(I32), w4_src[:, :, c4])
+            nc.sync.dma_start(w4_t[c0][:].bitcast(I32), w4_src[:, :, c0 // 2 : c1 // 2])
             nc.sync.dma_start(r8_t[c0][:].bitcast(I32), r8_src[:, :, c0:c1])
 
-        load_scales(nc.scalar, 0, EARLY)
+        def load_columns(tile, src, c0, c1):
+            nc.sync.dma_start(tile[:, c0:c1], src[:, c0:c1])
+
         nc.sync.dma_start(offs_t[:], offs)
-        nc.sync.dma_start(wgt_t[0], wgt[:, 0:HALF])
-        nc.sync.dma_start(planes[0][0][:], x_rows[0, 0])
-        nc.sync.dma_start(wgt_t[1], wgt[:, HALF:S])
-        for i in range(1, PACK):
-            nc.sync.dma_start(planes[0][i][:], x_rows[0, i])
+        load_columns(wgt_t, wgt, 0, HALF)
+        for n in range(PLANES):
+            nc.sync.dma_start(planes[n][:], x_rows[n // PACK, n % PACK])
+            if n == 0:
+                load_columns(wgt_t, wgt, HALF, S)
+            if 3 <= n < 11:
+                load_scales(n - 3, 0, EARLY)
+            if n in BIAS_BEHIND:
+                piece = BIAS_BEHIND.index(n)
+                r0, r1 = BIAS_PIECES[piece]
+                nc.sync.dma_start(b_rows[piece][0 : r1 - r0, :], b.rearrange("(r p) -> r p", p=P)[r0:r1])
+        load_weights(*CHUNKS[0])
+        load_weights(*CHUNKS[1])
         nc.sync.dma_start(offs2_t[:], offs2)
-        nc.sync.dma_start(b_rows[0:ROWS, :], b.rearrange("(r p) -> r p", p=P))
-        for a in range(1, PASSES):
-            for i in range(PACK):
-                nc.sync.dma_start(planes[a][i][:], x_rows[a, i])
-        load_weights(0, EARLY)
-        nc.sync.dma_start(wgo_t[:, 0:HALF], wgo[:, 0:HALF])
-        load_scales(nc.sync, EARLY, M)
-        load_weights(EARLY, 2 * EARLY)
-        nc.sync.dma_start(wgo_t[:, HALF:S], wgo[:, HALF:S])
-        load_weights(2 * EARLY, M)
+        load_columns(wgo_t, wgo, *FRONT)
+        load_weights(*CHUNKS[2])
+        load_columns(wgo_t, wgo, *REST)
+        for piece in range(8):
+            load_scales(piece, EARLY, M)
+        load_weights(*CHUNKS[3])
 
-        nc.tensor.transpose(banks[7][:, 0:P], b_rows[:], ident[:])
-        nc.scalar.copy(bias[:], banks[7][:, 0:ROWS])
-        first_bias = grouped[last, 1][:, 0:2].bitcast(F32)
-        nc.scalar.copy(first_bias, banks[7][:, 0:1])
+        for piece, (r0, r1) in enumerate(BIAS_PIECES):
+            nc.tensor.transpose(banks[5 + piece][:, 0:P], b_rows[piece], ident[:])
+            if piece == 0:
+                nc.scalar.copy(first_bias, banks[5][:, 0:1])
+            nc.scalar.copy(bias[:, r0:r1], banks[5 + piece][:, 0 : r1 - r0])
 
-        def gather(a, i, h):
+        def picks(a, c0, c1):
+            if a < last:
+                return picked[a][:, :, c0:c1]
+            if c1 <= HALF:
+                return picked_front[:, :, c0:c1]
+            return picked_rest[:, :, c0 - HALF : c1 - HALF]
+
+        def gather(n, c0, c1):
             nc.vector.tensor_tensor(
-                picked[a, h][:, i * HALF : (i + 1) * HALF],
-                planes[a][i][:].indirect(offs_t[:, h * HALF_COLS : (h + 1) * HALF_COLS]),
-                wgt_t[h],
+                picks(n // PACK, c0, c1)[:, n % PACK, :],
+                planes[n][:].indirect(offs_t[:, c0 // 16 : c1 // 16]),
+                wgt_t[:, c0:c1],
                 MULT,
             )
 
-        def interleave(a, h):
+        def rounded(a, c0, c1):
+            if a < last:
+                return grouped[a][:, PACK * c0 : PACK * c1]
+            part = FRONT if c1 <= HALF else REST
+            return grouped_last[part][:, PACK * (c0 - part[0]) : PACK * (c1 - part[0])]
+
+        def interleave(a, c0, c1):
             nc.scalar.copy(
-                grouped[a, h].rearrange("p (c j i) -> p c i j", j=4, i=PACK),
-                picked[a, h].rearrange("p (i c j) -> p c i j", j=4, i=PACK),
+                rounded(a, c0, c1).rearrange("p (c j i) -> p c i j", j=4, i=PACK),
+                picks(a, c0, c1).rearrange("p i (c j) -> p c i j", j=4),
             )
 
-        def quantize(a, c0, c1, src):
-            nc.vector.quantize_mx(out=codes[a][:, c0:c1].bitcast(FP8X4), scales=scales[a][:, c0:c1], in_=src)
+        def quantize(a, c0, c1):
+            nc.vector.quantize_mx(
+                out=codes[a][:, c0:c1].bitcast(FP8X4), scales=scales[a][:, c0:c1], in_=rounded(a, c0, c1)
+            )
 
-        def multiply(dst, r, a, c0, c1):
+        def multiply(r, a, c0, c1, bank):
+            chunk = max(c for c, end in CHUNKS if c <= P * r)
+            n0 = P * r - chunk
             base = 0 if P * r < EARLY else EARLY
             cols = slice(P * r - base, P * (r + 1) - base)
-            chunk = max(c0 for c0, c1 in chunks if c0 <= P * r)
-            n0 = P * r - chunk
-            for kind in range(2):
-                if kind == 0:
-                    lhsT = w4_t[chunk][:, a, 2 * n0 : 2 * (n0 + P)].bitcast(FP4X4)
-                    lhsT_scale = w_s[base][:, a, cols]
-                else:
-                    lhsT = r8_t[chunk][:, a, 4 * n0 : 4 * (n0 + P)].bitcast(FP8X4)
-                    lhsT_scale = w_s[base][4:P, a, cols]
+            w4_width = S if c1 - c0 == S else QUARTER
+            steps = [(r8_t[chunk][:, a, 4 * n0 : 4 * (n0 + P)].bitcast(FP8X4), w_s[base][4:P, a, cols], c0, c1)]
+            for c in range(c0, c1, w4_width):
+                steps.append((w4_t[chunk][:, a, 2 * n0 : 2 * (n0 + P)].bitcast(FP4X4), w_s[base][:, a, cols], c, c + w4_width))
+            for k, (lhsT, lhsT_scale, d0, d1) in enumerate(steps):
                 nc.tensor.matmul_mx(
-                    out=dst,
+                    out=bank[:, d0 - c0 : d1 - c0],
                     lhsT=lhsT,
                     lhsT_scale=lhsT_scale,
-                    rhs=codes[a][:, c0:c1].bitcast(FP8X4),
-                    rhs_scale=scales[a][:, c0:c1],
-                    start=(a == 0 and kind == 0),
-                    stop=(a == last and kind == 1),
+                    rhs=codes[a][:, d0:d1].bitcast(FP8X4),
+                    rhs_scale=scales[a][:, d0:d1],
+                    start=(a == 0 and k == 0),
+                    stop=(a == last and k == len(steps) - 1),
                 )
 
-        def multiply_open(h, a):
-            for q in (2 * h, 2 * h + 1):
-                multiply(banks[q][:, 0:QUARTER], 0, a, q * QUARTER, (q + 1) * QUARTER)
+        def finish(r, c0, c1, bank):
+            column = first_bias if (r, c0) == (0, 0) else bias[:, r : r + 1]
+            nc.scalar.activation(acts[r][:, c0:c1], bank[:, 0 : c1 - c0], SILU, bias=column)
 
-        def activate(r, c0, src):
-            c1 = c0 + src.shape[1]
-            column = first_bias if r == 0 and c1 <= HALF else bias[:, r : r + 1]
-            nc.scalar.activation(acts[r][:, c0:c1], src, SILU, bias=column)
-
-        def store(r):
-            nc.sync.dma_start(out[P * r : P * (r + 1), :], windows[r % WINDOWS][:])
-
-        def scatter_half(r, h):
-            cols = slice(h * HALF, (h + 1) * HALF)
+        def scatter(r, c0, c1):
+            window = windows[r % WINDOWS]
             nc.vector.tensor_tensor(
-                windows[r % WINDOWS][:].indirect(offs2_t[:, h * HALF_COLS : (h + 1) * HALF_COLS]),
-                acts[r][:, cols],
-                wgo_t[:, cols],
-                MULT,
+                window[:].indirect(offs2_t[:, c0 // 16 : c1 // 16]), acts[r][:, c0:c1], wgo_t[:, c0:c1], MULT
             )
+            if c1 == S:
+                nc.sync.dma_start(out[P * r : P * (r + 1), :], window[:])
 
-        def late(r, dst, c0, c1):
-            for a in range(PASSES):
-                multiply(dst, r, a, c0, c1)
-
-        def late_half(r, h, bank):
-            for k in range(2):
-                late(r, bank[:, k * QUARTER : (k + 1) * QUARTER], h * HALF + k * QUARTER, h * HALF + (k + 1) * QUARTER)
-            activate(r, h * HALF, bank[:, 0:HALF])
-
+        for n in range(last * PACK):
+            if n in (0, last * PACK - 1):
+                gather(n, *FRONT)
+                gather(n, *REST)
+            else:
+                gather(n, *WHOLE)
+            if n % PACK == PACK - 1:
+                interleave(n // PACK, *FRONT)
+                interleave(n // PACK, *REST)
+        codes[0] = held.tile([P, S], U32, name="codes0", tag="b_rows0", align_bytes=64)
+        quantize(0, *WHOLE)
+        for n in range(last * PACK, PLANES - 1):
+            gather(n, *FRONT)
+        codes[1] = held.tile([P, S], U32, name="codes1", tag="b_rows1", align_bytes=64)
+        quantize(1, *WHOLE)
+        for c0 in (0, QUARTER):
+            gather(PLANES - 1, c0, c0 + QUARTER)
+            interleave(last, c0, c0 + QUARTER)
         for a in range(last):
-            for i in range(PACK):
-                for h in range(2):
-                    gather(a, i, h)
-                    if i == PACK - 1:
-                        interleave(a, h)
-        for i in range(PACK):
-            gather(last, i, 0)
-        interleave(last, 0)
-        codes[0] = held.tile([P, S], U32, name="codes0", tag="x1_1", align_bytes=64)
-        quantize(0, 0, S, grouped[0])
-        for h in range(2):
-            quantize(1, h * HALF, (h + 1) * HALF, grouped[1, h])
-        for a in range(last):
-            multiply_open(0, a)
-        for i in range(2):
-            gather(last, i, 1)
-        quantize(last, 0, HALF, grouped[last, 0])
-        multiply_open(0, last)
-        for i in range(2, PACK):
-            gather(last, i, 1)
-        for q in range(2):
-            activate(0, q * QUARTER, banks[q][:, 0:QUARTER])
-        interleave(last, 1)
-        scatter_half(0, 0)
-        late_half(1, 0, banks[4])
-        for a in range(last):
-            multiply_open(1, a)
-        quantize(last, HALF, S, grouped[last, 1])
-        multiply_open(1, last)
-        for q in range(2, 4):
-            activate(0, q * QUARTER, banks[q][:, 0:QUARTER])
-        scatter_half(1, 0)
-        scatter_half(0, 1)
-        store(0)
-        late_half(1, 1, banks[5])
-        scatter_half(1, 1)
-        store(1)
+            multiply(0, a, *FRONT, banks[0])
+        for n in range(last * PACK, last * PACK + 2):
+            gather(n, *REST)
+        quantize(last, *FRONT)
+        multiply(0, last, *FRONT, banks[0])
+        for n in range(last * PACK + 2, PLANES):
+            gather(n, *REST)
+        finish(0, *FRONT, banks[0])
+        interleave(last, *REST)
+        scatter(0, *FRONT)
+        for a in range(PASSES):
+            multiply(1, a, *FRONT, banks[1])
+        finish(1, *FRONT, banks[1])
+        for r in range(2):
+            for a in range(last):
+                multiply(r, a, *REST, banks[2 + r])
+        quantize(last, *REST)
+        multiply(0, last, *REST, banks[2])
+        finish(0, *REST, banks[2])
+        scatter(1, *FRONT)
+        scatter(0, *REST)
+        multiply(1, last, *REST, banks[3])
+        finish(1, *REST, banks[3])
+        scatter(1, *REST)
         for r in range(2, ROWS):
-            bank = banks[(0, 1, 4, 2, 3, 5)[r - 2]]
-            late(r, bank[:], 0, S)
-            activate(r, 0, bank[:])
-            nc.vector.tensor_tensor(windows[r % WINDOWS][:].indirect(offs2_t[:]), acts[r][:], wgo_t[:], MULT)
-            store(r)
+            bank = banks[(r, r - 4)[r >= 4]]
+            for a in range(PASSES):
+                multiply(r, a, *WHOLE, bank)
+            finish(r, *WHOLE, bank)
+            scatter(r, *WHOLE)

@@ -23,8 +23,8 @@ ROWS = M // P
 HALF = S // 2
 QUARTER = S // 4
 WINDOWS = 3
-EARLY = 2 * P
-CHUNKS = ((0, P), (P, 2 * P), (2 * P, 4 * P), (4 * P, M))
+EARLY = 3 * P
+CHUNKS = ((0, P), (P, 2 * P), (2 * P, 3 * P), (3 * P, 5 * P), (5 * P, M))
 FRONT, REST, WHOLE = (0, HALF), (HALF, S), (0, S)
 BIAS_PIECES = ((0, 2), (2, 4), (4, 8))
 BIAS_BEHIND = (6, 10, 11)
@@ -89,11 +89,11 @@ def tile_list_hboth_silu_kernel(
         nc.scalar.activation(dummy[:, 1:2], dummy[:, 0:1], SILU)
 
         def load_scales(piece, c0, c1):
-            q, kind = divmod(piece, 2)
+            r, kind = divmod(piece, 2)
             first, src = ((0, w4_scales), (4, r8_scales))[kind]
             nc.sync.dma_start(
-                w_s[c0][32 * q + first : 32 * q + first + 4].bitcast(I32),
-                src[:, 4 * q : 4 * q + 4, c0:c1].bitcast(I32).rearrange("a r n -> r a n"),
+                w_s[c0][first + r : P : 32].bitcast(I32),
+                src[:, :, c0:c1].bitcast(I32).rearrange("a (q r) n -> r q a n", r=4)[r],
             )
 
         def load_weights(c0, c1):
@@ -124,6 +124,7 @@ def tile_list_hboth_silu_kernel(
         for piece in range(8):
             load_scales(piece, EARLY, M)
         load_weights(*CHUNKS[3])
+        load_weights(*CHUNKS[4])
 
         for piece, (r0, r1) in enumerate(BIAS_PIECES):
             nc.tensor.transpose(banks[5 + piece][:, 0:P], b_rows[piece], ident[:])
@@ -239,7 +240,7 @@ def tile_list_hboth_silu_kernel(
         finish(1, *REST, banks[3])
         scatter(1, *REST)
         for r in range(2, ROWS):
-            bank = banks[(r, r - 4)[r >= 4]]
+            bank = banks[(r + 2) % 8]
             for a in range(PASSES):
                 multiply(r, a, *WHOLE, bank)
             finish(r, *WHOLE, bank)

@@ -18,16 +18,23 @@ K, M, T, S = 1536, 1024, 1024, 512
 P = 128
 PACK = 4
 PASSES = K // (P * PACK)
+LAST = PASSES - 1
 PLANES = PASSES * PACK
-ROWS = M // P
+ROW_TILES = M // P
 HALF = S // 2
 QUARTER = S // 4
-WINDOWS = 3
-EARLY = 3 * P
-CHUNKS = ((0, P), (P, 2 * P), (2 * P, 3 * P), (3 * P, 5 * P), (5 * P, M))
 FRONT, REST, WHOLE = (0, HALF), (HALF, S), (0, S)
+W4, R8 = 0, 1
+SCALE_ROWS = 4
+SCALE_START = {W4: 0, R8: SCALE_ROWS}
+WINDOWS = 3
+CHUNKS = ((0, P), (P, 2 * P), (2 * P, 3 * P), (3 * P, 5 * P), (5 * P, M))
+EARLY = 3 * P
 BIAS_PIECES = ((0, 2), (2, 4), (4, 8))
 BIAS_BEHIND = (6, 10, 11)
+BIAS_BANK = 5
+LATE_BIAS = BIAS_PIECES[2][0]
+SCALES_BEHIND = 7
 FLOPS = 2 * 2 * K * M * S
 
 
@@ -35,109 +42,131 @@ def tile_list_hboth_silu_kernel(
     tc, xT, w4_words, w4_scales, r8_words, r8_scales, wgt, b, wgo, offs, offs2, out
 ):
     nc = tc.nc
-    last = PASSES - 1
     with ExitStack() as ctx:
-        held = ctx.enter_context(tc.tile_pool(name="held", bufs=1))
+        pool = ctx.enter_context(tc.tile_pool(name="pool", bufs=1))
         psum = ctx.enter_context(tc.psum_pool(name="psum", bufs=1))
 
-        offs_t = held.tile([P, S // 16], U16, name="offs_t")
-        offs2_t = held.tile([P, S // 16], U16, name="offs2_t")
-        wgt_t = held.tile([P, S], F32, name="wgt_t")
-        wgo_t = held.tile([P, S], F32, name="wgo_t")
-        planes = [held.tile([P, T], F32, name=f"x{n}", tag=f"x{n}", align_bytes=64) for n in range(PLANES)]
+        offs_t = pool.tile([P, S // 16], U16, name="offs_t")
+        offs2_t = pool.tile([P, S // 16], U16, name="offs2_t")
+        wgt_t = pool.tile([P, S], F32, name="wgt_t")
+        wgo_t = pool.tile([P, S], F32, name="wgo_t")
+        planes = [pool.tile([P, T], F32, name=f"plane{n}", align_bytes=64) for n in range(PLANES)]
         picked = [
-            held.tile([P, PACK * S], F32, name=f"picked{a}")[:].rearrange("p (i s) -> p i s", i=PACK) for a in range(last)
+            pool.tile([P, PACK * S], F32, name=f"picked{a}")[:].rearrange("p (i s) -> p i s", i=PACK)
+            for a in range(LAST)
         ]
-        grouped = [held.tile([P, S * PACK], BF16, name=f"grouped{a}", align_bytes=64) for a in range(last)]
-        shared = held.tile([P, 6 * HALF], F32, name="shared")
+        grouped = [pool.tile([P, S * PACK], BF16, name=f"grouped{a}", align_bytes=64) for a in range(LAST)]
+        shared = pool.tile([P, 6 * HALF], F32, name="shared")
         picked_front = shared[:, 2 * HALF : 6 * HALF].rearrange("p (i s) -> p i s", i=PACK)
         picked_rest = shared[:, 0 : 4 * HALF].rearrange("p (i s) -> p i s", i=PACK)
         grouped_last = {
-            part: held.tile([P, HALF * PACK], BF16, name=f"grouped_last{part[0]}", align_bytes=64) for part in (FRONT, REST)
+            part: pool.tile([P, HALF * PACK], BF16, name=f"grouped_last{part[0]}", align_bytes=64)
+            for part in (FRONT, REST)
         }
-        codes = {last: held.tile([P, S], U32, name="codes_last", align_bytes=64)}
-        scales = [held.tile([P, S], U8, name=f"scales{a}", align_bytes=64) for a in range(PASSES)]
-        w4_t = {c0: held.tile([P, PASSES, 2 * (c1 - c0)], U8, name=f"w4_{c0}", align_bytes=64) for c0, c1 in CHUNKS}
-        r8_t = {c0: held.tile([P, PASSES, 4 * (c1 - c0)], U8, name=f"r8_{c0}", align_bytes=64) for c0, c1 in CHUNKS}
-        w_s = {
-            0: held.tile([P, PASSES, EARLY], U8, name="scales_early", align_bytes=64),
-            EARLY: held.tile([P, PASSES, M - EARLY], U8, name="scales_late", align_bytes=64),
+        codes = {LAST: pool.tile([P, S], U32, name="codes_last", align_bytes=64)}
+        scales = [pool.tile([P, S], U8, name=f"scales{a}", align_bytes=64) for a in range(PASSES)]
+        w4_t = {c0: pool.tile([P, PASSES, 2 * (c1 - c0)], U8, name=f"w4_{c0}", align_bytes=64) for c0, c1 in CHUNKS}
+        r8_t = {c0: pool.tile([P, PASSES, 4 * (c1 - c0)], U8, name=f"r8_{c0}", align_bytes=64) for c0, c1 in CHUNKS}
+        w4_scales_early = pool.tile([P, PASSES, EARLY], U8, name="w4_scales_early", align_bytes=64)
+        scales_late = pool.tile([P, PASSES, M - EARLY], U8, name="scales_late", align_bytes=64)
+        r8_scales_early = pool.tile([P, PASSES, EARLY], U8, name="r8_scales_early", align_bytes=64)
+        weight_scales = {
+            (W4, 0): w4_scales_early,
+            (R8, 0): r8_scales_early,
+            (W4, EARLY): scales_late,
+            (R8, EARLY): scales_late,
         }
-        windows = [held.tile([P, T], F32, name=f"window{w}") for w in range(WINDOWS)]
-        acts = [held.tile([P, S], F32, name=f"act{r}") for r in range(ROWS)]
-        b_rows = [held.tile([P, P], F32, name=f"b_rows{k}", tag=f"b_rows{k}", align_bytes=64)[:] for k in range(2)]
+        windows = [pool.tile([P, T], F32, name=f"window{w}") for w in range(WINDOWS)]
+        acts = [pool.tile([P, S], F32, name=f"act{r}") for r in range(ROW_TILES)]
+        b_rows = [pool.tile([P, P], F32, name=f"b_rows{k}", tag=f"b_rows{k}", align_bytes=64)[:] for k in range(2)]
         b_rows.append(shared[:, HALF - P // 2 : HALF + P // 2])
-        ident = held.tile([P, P], F32, name="ident")
-        bias = held.tile([P, ROWS], F32, name="bias")
+        ident = pool.tile([P, P], F32, name="ident")
+        bias = pool.tile([P, LATE_BIAS], F32, name="bias")
+        late_bias = shared[:, 6 * HALF - (ROW_TILES - LATE_BIAS) : 6 * HALF]
         first_bias = grouped_last[REST][:, 0:2].bitcast(F32)
-        dummy = held.tile([P, 2], F32, name="dummy")
-        banks = [psum.tile([P, 512], F32, name=f"bank{k}") for k in range(8)]
+        banks = [psum.tile([P, S], F32, name=f"bank{k}") for k in range(8)]
 
         x_rows = xT.rearrange("(a p i) t -> a i p t", p=P, i=PACK)
+        b_by_tile = b.rearrange("(r p) -> r p", p=P)
         w4_src = w4_words.bitcast(I32).rearrange("a p c -> p a c")
         r8_src = r8_words.rearrange("a p n i -> a p (n i)").bitcast(I32).rearrange("a p c -> p a c")
 
-        nc.gpsimd.memset(dummy[:], 0.0)
-        nc.vector.memset(w_s[0][:].bitcast(I32), 0)
+        nc.vector.memset(w4_scales_early[:].bitcast(I32), 0)
         nc.vector.memset(windows[0][:], 0.0)
-        for rows in b_rows:
+        for rows in b_rows[1:]:
             nc.gpsimd.memset(rows, 0.0)
+        nc.scalar.activation(b_rows[0], b_rows[1], SILU)
         make_identity(nc, ident[:])
-        nc.gpsimd.memset(w_s[EARLY][:].bitcast(I32), 0)
+        nc.gpsimd.memset(r8_scales_early[:].bitcast(I32), 0)
+        nc.gpsimd.memset(scales_late[:].bitcast(I32), 0)
         for w in range(1, WINDOWS):
             nc.gpsimd.memset(windows[w][:], 0.0)
-        nc.scalar.activation(dummy[:, 1:2], dummy[:, 0:1], SILU)
 
-        def load_scales(piece, c0, c1):
-            r, kind = divmod(piece, 2)
-            first, src = ((0, w4_scales), (4, r8_scales))[kind]
+        def load_scales(kind, r, c0, c1):
+            src = (w4_scales, r8_scales)[kind]
             nc.sync.dma_start(
-                w_s[c0][first + r : P : 32].bitcast(I32),
-                src[:, :, c0:c1].bitcast(I32).rearrange("a (q r) n -> r q a n", r=4)[r],
+                weight_scales[kind, c0][SCALE_START[kind] + r : P : 32].bitcast(I32),
+                src[:, :, c0:c1].bitcast(I32).rearrange("a (q r) n -> r q a n", r=SCALE_ROWS)[r],
             )
 
-        def load_weights(c0, c1):
+        def load_w4(c0, c1):
             nc.sync.dma_start(w4_t[c0][:].bitcast(I32), w4_src[:, :, c0 // 2 : c1 // 2])
+
+        def load_r8(c0, c1):
             nc.sync.dma_start(r8_t[c0][:].bitcast(I32), r8_src[:, :, c0:c1])
+
+        def load_weights(c0, c1):
+            load_w4(c0, c1)
+            load_r8(c0, c1)
 
         def load_columns(tile, src, c0, c1):
             nc.sync.dma_start(tile[:, c0:c1], src[:, c0:c1])
 
         nc.sync.dma_start(offs_t[:], offs)
-        load_columns(wgt_t, wgt, 0, HALF)
+        load_columns(wgt_t, wgt, *FRONT)
         for n in range(PLANES):
             nc.sync.dma_start(planes[n][:], x_rows[n // PACK, n % PACK])
             if n == 0:
-                load_columns(wgt_t, wgt, HALF, S)
-            if 3 <= n < 11:
-                load_scales(n - 3, 0, EARLY)
+                load_columns(wgt_t, wgt, *REST)
+            if SCALES_BEHIND <= n < SCALES_BEHIND + SCALE_ROWS:
+                load_scales(W4, n - SCALES_BEHIND, 0, EARLY)
             if n in BIAS_BEHIND:
                 piece = BIAS_BEHIND.index(n)
                 r0, r1 = BIAS_PIECES[piece]
-                nc.sync.dma_start(b_rows[piece][0 : r1 - r0, :], b.rearrange("(r p) -> r p", p=P)[r0:r1])
-        load_weights(*CHUNKS[0])
+                nc.sync.dma_start(b_rows[piece][0 : r1 - r0, :], b_by_tile[r0:r1])
+        load_w4(*CHUNKS[0])
+        for r in range(SCALE_ROWS):
+            load_scales(R8, r, 0, EARLY)
+        load_r8(*CHUNKS[0])
         load_weights(*CHUNKS[1])
         nc.sync.dma_start(offs2_t[:], offs2)
         load_columns(wgo_t, wgo, *FRONT)
         load_weights(*CHUNKS[2])
         load_columns(wgo_t, wgo, *REST)
-        for piece in range(8):
-            load_scales(piece, EARLY, M)
+        for r in range(SCALE_ROWS):
+            for kind in (W4, R8):
+                load_scales(kind, r, EARLY, M)
         load_weights(*CHUNKS[3])
         load_weights(*CHUNKS[4])
 
-        for piece, (r0, r1) in enumerate(BIAS_PIECES):
-            nc.tensor.transpose(banks[5 + piece][:, 0:P], b_rows[piece], ident[:])
-            if piece == 0:
-                nc.scalar.copy(first_bias, banks[5][:, 0:1])
-            nc.scalar.copy(bias[:, r0:r1], banks[5 + piece][:, 0 : r1 - r0])
+        for piece in range(len(BIAS_PIECES)):
+            nc.tensor.transpose(banks[BIAS_BANK + piece][:, 0:P], b_rows[piece], ident[:])
+        nc.scalar.copy(first_bias, banks[BIAS_BANK][:, 0:1])
+        for piece, (r0, r1) in enumerate(BIAS_PIECES[:2]):
+            nc.scalar.copy(bias[:, r0:r1], banks[BIAS_BANK + piece][:, 0 : r1 - r0])
 
         def picks(a, c0, c1):
-            if a < last:
+            if a < LAST:
                 return picked[a][:, :, c0:c1]
             if c1 <= HALF:
                 return picked_front[:, :, c0:c1]
             return picked_rest[:, :, c0 - HALF : c1 - HALF]
+
+        def rounded(a, c0, c1):
+            if a < LAST:
+                return grouped[a][:, PACK * c0 : PACK * c1]
+            part = FRONT if c1 <= HALF else REST
+            return grouped_last[part][:, PACK * (c0 - part[0]) : PACK * (c1 - part[0])]
 
         def gather(n, c0, c1):
             nc.vector.tensor_tensor(
@@ -146,12 +175,6 @@ def tile_list_hboth_silu_kernel(
                 wgt_t[:, c0:c1],
                 MULT,
             )
-
-        def rounded(a, c0, c1):
-            if a < last:
-                return grouped[a][:, PACK * c0 : PACK * c1]
-            part = FRONT if c1 <= HALF else REST
-            return grouped_last[part][:, PACK * (c0 - part[0]) : PACK * (c1 - part[0])]
 
         def interleave(a, c0, c1):
             nc.scalar.copy(
@@ -164,28 +187,44 @@ def tile_list_hboth_silu_kernel(
                 out=codes[a][:, c0:c1].bitcast(FP8X4), scales=scales[a][:, c0:c1], in_=rounded(a, c0, c1)
             )
 
-        def multiply(r, a, c0, c1, bank):
-            chunk = max(c for c, end in CHUNKS if c <= P * r)
+        def multiply(r, a, kind, c0, c1, bank):
+            chunk = max(start for start, end in CHUNKS if start <= P * r)
             n0 = P * r - chunk
             base = 0 if P * r < EARLY else EARLY
-            cols = slice(P * r - base, P * (r + 1) - base)
-            w4_width = S if c1 - c0 == S else QUARTER
-            steps = [(r8_t[chunk][:, a, 4 * n0 : 4 * (n0 + P)].bitcast(FP8X4), w_s[base][4:P, a, cols], c0, c1)]
-            for c in range(c0, c1, w4_width):
-                steps.append((w4_t[chunk][:, a, 2 * n0 : 2 * (n0 + P)].bitcast(FP4X4), w_s[base][:, a, cols], c, c + w4_width))
-            for k, (lhsT, lhsT_scale, d0, d1) in enumerate(steps):
+            lhsT_scale = weight_scales[kind, base][SCALE_START[kind] : P, a, P * r - base : P * (r + 1) - base]
+            if kind == W4:
+                lhsT = w4_t[chunk][:, a, 2 * n0 : 2 * (n0 + P)].bitcast(FP4X4)
+                width = S if c1 - c0 == S else QUARTER
+            else:
+                lhsT = r8_t[chunk][:, a, 4 * n0 : 4 * (n0 + P)].bitcast(FP8X4)
+                width = c1 - c0
+            for c in range(c0, c1, width):
                 nc.tensor.matmul_mx(
-                    out=bank[:, d0 - c0 : d1 - c0],
+                    out=bank[:, c - c0 : c - c0 + width],
                     lhsT=lhsT,
                     lhsT_scale=lhsT_scale,
-                    rhs=codes[a][:, d0:d1].bitcast(FP8X4),
-                    rhs_scale=scales[a][:, d0:d1],
-                    start=(a == 0 and k == 0),
-                    stop=(a == last and k == len(steps) - 1),
+                    rhs=codes[a][:, c : c + width].bitcast(FP8X4),
+                    rhs_scale=scales[a][:, c : c + width],
+                    start=((a, kind, c) == (0, W4, c0)),
+                    stop=((a, kind) == (LAST, R8)),
                 )
 
-        def finish(r, c0, c1, bank):
-            column = first_bias if (r, c0) == (0, 0) else bias[:, r : r + 1]
+        def multiply_early(r, c0, c1, bank):
+            for kind in (W4, R8):
+                for a in range(LAST):
+                    multiply(r, a, kind, c0, c1, bank)
+
+        def multiply_last(r, c0, c1, bank):
+            for kind in (W4, R8):
+                multiply(r, LAST, kind, c0, c1, bank)
+
+        def activate(r, c0, c1, bank):
+            if (r, c0) == (0, 0):
+                column = first_bias
+            elif r < LATE_BIAS:
+                column = bias[:, r : r + 1]
+            else:
+                column = late_bias[:, r - LATE_BIAS : r - LATE_BIAS + 1]
             nc.scalar.activation(acts[r][:, c0:c1], bank[:, 0 : c1 - c0], SILU, bias=column)
 
         def scatter(r, c0, c1):
@@ -196,8 +235,9 @@ def tile_list_hboth_silu_kernel(
             if c1 == S:
                 nc.sync.dma_start(out[P * r : P * (r + 1), :], window[:])
 
-        for n in range(last * PACK):
-            if n in (0, last * PACK - 1):
+        first_of_last = LAST * PACK
+        for n in range(first_of_last):
+            if n in (0, first_of_last - 1):
                 gather(n, *FRONT)
                 gather(n, *REST)
             else:
@@ -205,43 +245,45 @@ def tile_list_hboth_silu_kernel(
             if n % PACK == PACK - 1:
                 interleave(n // PACK, *FRONT)
                 interleave(n // PACK, *REST)
-        codes[0] = held.tile([P, S], U32, name="codes0", tag="b_rows0", align_bytes=64)
+        codes[0] = pool.tile([P, S], U32, name="codes0", tag="b_rows0", align_bytes=64)
         quantize(0, *WHOLE)
-        for n in range(last * PACK, PLANES - 1):
+
+        for n in range(first_of_last, PLANES - 1):
             gather(n, *FRONT)
-        codes[1] = held.tile([P, S], U32, name="codes1", tag="b_rows1", align_bytes=64)
+        codes[1] = pool.tile([P, S], U32, name="codes1", tag="b_rows1", align_bytes=64)
         quantize(1, *WHOLE)
         for c0 in (0, QUARTER):
             gather(PLANES - 1, c0, c0 + QUARTER)
-            interleave(last, c0, c0 + QUARTER)
-        for a in range(last):
-            multiply(0, a, *FRONT, banks[0])
-        for n in range(last * PACK, last * PACK + 2):
+            interleave(LAST, c0, c0 + QUARTER)
+        nc.scalar.copy(late_bias, banks[BIAS_BANK + 2][:, 0 : ROW_TILES - LATE_BIAS])
+        multiply_early(0, *FRONT, banks[0])
+        for n in range(first_of_last, first_of_last + 2):
             gather(n, *REST)
-        quantize(last, *FRONT)
-        multiply(0, last, *FRONT, banks[0])
-        for n in range(last * PACK + 2, PLANES):
+        quantize(LAST, *FRONT)
+        multiply_last(0, *FRONT, banks[0])
+        for n in range(first_of_last + 2, PLANES):
             gather(n, *REST)
-        finish(0, *FRONT, banks[0])
-        interleave(last, *REST)
+        activate(0, *FRONT, banks[0])
+        interleave(LAST, *REST)
+
         scatter(0, *FRONT)
-        for a in range(PASSES):
-            multiply(1, a, *FRONT, banks[1])
-        finish(1, *FRONT, banks[1])
+        multiply_early(1, *FRONT, banks[1])
+        multiply_last(1, *FRONT, banks[1])
+        activate(1, *FRONT, banks[1])
         for r in range(2):
-            for a in range(last):
-                multiply(r, a, *REST, banks[2 + r])
-        quantize(last, *REST)
-        multiply(0, last, *REST, banks[2])
-        finish(0, *REST, banks[2])
+            multiply_early(r, *REST, banks[2 + r])
+        quantize(LAST, *REST)
+        multiply_last(0, *REST, banks[2])
+        activate(0, *REST, banks[2])
         scatter(1, *FRONT)
         scatter(0, *REST)
-        multiply(1, last, *REST, banks[3])
-        finish(1, *REST, banks[3])
+        multiply_last(1, *REST, banks[3])
+        activate(1, *REST, banks[3])
         scatter(1, *REST)
-        for r in range(2, ROWS):
-            bank = banks[(r + 2) % 8]
-            for a in range(PASSES):
-                multiply(r, a, *WHOLE, bank)
-            finish(r, *WHOLE, bank)
+
+        for r in range(2, ROW_TILES):
+            bank = banks[(r + 2) % len(banks)]
+            multiply_early(r, *WHOLE, bank)
+            multiply_last(r, *WHOLE, bank)
+            activate(r, *WHOLE, bank)
             scatter(r, *WHOLE)

@@ -30,10 +30,13 @@ SCALE_START = {W4: 0, R8: SCALE_ROWS}
 WINDOWS = 3
 CHUNKS = ((0, P), (P, 2 * P), (2 * P, 3 * P), (3 * P, 5 * P), (5 * P, M))
 EARLY = 3 * P
-BIAS_PIECES = ((0, 2), (2, 4), (4, 8))
-BIAS_BEHIND = (6, 10, 11)
-BIAS_BANK = 5
-LATE_BIAS = BIAS_PIECES[2][0]
+BIAS_PIECES = ((0, 4), (4, 8))
+BIAS_BEHIND = (6, 11)
+BIAS_BANK = 6
+LATE_BIAS = BIAS_PIECES[1][0]
+REST_STEP = S + 3 * S // 8
+BY_PASS = [(a, kind) for a in range(PASSES) for kind in (W4, R8)]
+BY_LOAD = [(a, kind) for kind in (W4, R8) for a in range(LAST)] + [(LAST, W4), (LAST, R8)]
 SCALES_BEHIND = 7
 FLOPS = 2 * 2 * K * M * S
 
@@ -56,9 +59,9 @@ def tile_list_hboth_silu_kernel(
             for a in range(LAST)
         ]
         grouped = [pool.tile([P, S * PACK], BF16, name=f"grouped{a}", align_bytes=64) for a in range(LAST)]
-        shared = pool.tile([P, 6 * HALF], F32, name="shared")
-        picked_front = shared[:, 2 * HALF : 6 * HALF].rearrange("p (i s) -> p i s", i=PACK)
-        picked_rest = shared[:, 0 : 4 * HALF].rearrange("p (i s) -> p i s", i=PACK)
+        shared = pool.tile([P, HALF + PACK * REST_STEP], F32, name="shared")
+        picked_front = shared[:, 0 : PACK * S].rearrange("p (i s) -> p i s", i=PACK)
+        picked_rest = shared[:, HALF:].rearrange("p (i s) -> p i s", i=PACK)
         grouped_last = {
             part: pool.tile([P, HALF * PACK], BF16, name=f"grouped_last{part[0]}", align_bytes=64)
             for part in (FRONT, REST)
@@ -78,11 +81,11 @@ def tile_list_hboth_silu_kernel(
         }
         windows = [pool.tile([P, T], F32, name=f"window{w}") for w in range(WINDOWS)]
         acts = [pool.tile([P, S], F32, name=f"act{r}") for r in range(ROW_TILES)]
-        b_rows = [pool.tile([P, P], F32, name=f"b_rows{k}", tag=f"b_rows{k}", align_bytes=64)[:] for k in range(2)]
-        b_rows.append(shared[:, HALF - P // 2 : HALF + P // 2])
-        ident = pool.tile([P, P], F32, name="ident")
+        b_rows = [pool.tile([P, P], F32, name=f"b_rows{k}", tag=f"b_rows{k}", align_bytes=64)[:] for k in range(1)]
+        b_rows.append(picked_rest[:, PACK - 1, 0:P])
+        ident = pool.tile([P, P], F32, name="ident", tag="ident", align_bytes=64)
         bias = pool.tile([P, LATE_BIAS], F32, name="bias")
-        late_bias = shared[:, 6 * HALF - (ROW_TILES - LATE_BIAS) : 6 * HALF]
+        late_bias = shared[:, HALF - (ROW_TILES - LATE_BIAS) : HALF]
         first_bias = grouped_last[REST][:, 0:2].bitcast(F32)
         banks = [psum.tile([P, S], F32, name=f"bank{k}") for k in range(8)]
 
@@ -152,13 +155,13 @@ def tile_list_hboth_silu_kernel(
         for piece in range(len(BIAS_PIECES)):
             nc.tensor.transpose(banks[BIAS_BANK + piece][:, 0:P], b_rows[piece], ident[:])
         nc.scalar.copy(first_bias, banks[BIAS_BANK][:, 0:1])
-        for piece, (r0, r1) in enumerate(BIAS_PIECES[:2]):
+        for piece, (r0, r1) in enumerate(BIAS_PIECES[:1]):
             nc.scalar.copy(bias[:, r0:r1], banks[BIAS_BANK + piece][:, 0 : r1 - r0])
 
         def picks(a, c0, c1):
             if a < LAST:
                 return picked[a][:, :, c0:c1]
-            if c1 <= HALF:
+            if c0 < HALF:
                 return picked_front[:, :, c0:c1]
             return picked_rest[:, :, c0 - HALF : c1 - HALF]
 
@@ -209,14 +212,9 @@ def tile_list_hboth_silu_kernel(
                     stop=((a, kind) == (LAST, R8)),
                 )
 
-        def multiply_early(r, c0, c1, bank):
-            for kind in (W4, R8):
-                for a in range(LAST):
-                    multiply(r, a, kind, c0, c1, bank)
-
-        def multiply_last(r, c0, c1, bank):
-            for kind in (W4, R8):
-                multiply(r, LAST, kind, c0, c1, bank)
+        def multiply_group(r, c0, c1, bank, order):
+            for a, kind in order:
+                multiply(r, a, kind, c0, c1, bank)
 
         def activate(r, c0, c1, bank):
             if (r, c0) == (0, 0):
@@ -248,42 +246,39 @@ def tile_list_hboth_silu_kernel(
         codes[0] = pool.tile([P, S], U32, name="codes0", tag="b_rows0", align_bytes=64)
         quantize(0, *WHOLE)
 
-        for n in range(first_of_last, PLANES - 1):
+        gather(first_of_last, *WHOLE)
+        for n in range(first_of_last + 1, PLANES - 1):
             gather(n, *FRONT)
-        codes[1] = pool.tile([P, S], U32, name="codes1", tag="b_rows1", align_bytes=64)
-        quantize(1, *WHOLE)
         for c0 in (0, QUARTER):
             gather(PLANES - 1, c0, c0 + QUARTER)
             interleave(LAST, c0, c0 + QUARTER)
-        nc.scalar.copy(late_bias, banks[BIAS_BANK + 2][:, 0 : ROW_TILES - LATE_BIAS])
-        multiply_early(0, *FRONT, banks[0])
-        for n in range(first_of_last, first_of_last + 2):
-            gather(n, *REST)
+        nc.scalar.copy(late_bias, banks[BIAS_BANK + 1][:, 0 : ROW_TILES - LATE_BIAS])
+        codes[1] = pool.tile([P, S], U32, name="codes1", tag="ident", align_bytes=64)
+        quantize(1, *WHOLE)
+        gather(PLANES - 1, *REST)
         quantize(LAST, *FRONT)
-        multiply_last(0, *FRONT, banks[0])
-        for n in range(first_of_last + 2, PLANES):
+        multiply_group(0, *FRONT, banks[0], BY_PASS)
+        for n in range(first_of_last + 1, PLANES - 1):
             gather(n, *REST)
         activate(0, *FRONT, banks[0])
         interleave(LAST, *REST)
 
         scatter(0, *FRONT)
-        multiply_early(1, *FRONT, banks[1])
-        multiply_last(1, *FRONT, banks[1])
+        multiply_group(1, *FRONT, banks[1], BY_LOAD)
         activate(1, *FRONT, banks[1])
-        for r in range(2):
-            multiply_early(r, *REST, banks[2 + r])
+        multiply_group(0, *REST, banks[2], BY_PASS[:-2])
+        multiply_group(1, *REST, banks[3], BY_LOAD[:-2])
         quantize(LAST, *REST)
-        multiply_last(0, *REST, banks[2])
+        multiply_group(0, *REST, banks[2], BY_PASS[-2:])
         activate(0, *REST, banks[2])
         scatter(1, *FRONT)
         scatter(0, *REST)
-        multiply_last(1, *REST, banks[3])
+        multiply_group(1, *REST, banks[3], BY_LOAD[-2:])
         activate(1, *REST, banks[3])
         scatter(1, *REST)
 
         for r in range(2, ROW_TILES):
             bank = banks[(r + 2) % len(banks)]
-            multiply_early(r, *WHOLE, bank)
-            multiply_last(r, *WHOLE, bank)
+            multiply_group(r, *WHOLE, bank, BY_LOAD)
             activate(r, *WHOLE, bank)
             scatter(r, *WHOLE)

@@ -30,14 +30,14 @@ SCALE_START = {W4: 0, R8: SCALE_ROWS}
 WINDOWS = 3
 CHUNKS = ((0, P), (P, 2 * P), (2 * P, 3 * P), (3 * P, 5 * P), (5 * P, M))
 EARLY = 3 * P
-BIAS_PIECES = ((0, 4), (4, 8))
-BIAS_BEHIND = (6, 11)
+LATE_BIAS = ROW_TILES // 2
+BIAS_PIECES = ((0, LATE_BIAS), (LATE_BIAS, ROW_TILES))
+BIAS_BEHIND = (6, PLANES - 1)
 BIAS_BANK = 6
-LATE_BIAS = BIAS_PIECES[1][0]
+SCALES_BEHIND = 7
 REST_STEP = S + 3 * S // 8
 BY_PASS = [(a, kind) for a in range(PASSES) for kind in (W4, R8)]
 BY_LOAD = [(a, kind) for kind in (W4, R8) for a in range(LAST)] + [(LAST, W4), (LAST, R8)]
-SCALES_BEHIND = 7
 FLOPS = 2 * 2 * K * M * S
 
 
@@ -81,8 +81,10 @@ def tile_list_hboth_silu_kernel(
         }
         windows = [pool.tile([P, T], F32, name=f"window{w}") for w in range(WINDOWS)]
         acts = [pool.tile([P, S], F32, name=f"act{r}") for r in range(ROW_TILES)]
-        b_rows = [pool.tile([P, P], F32, name=f"b_rows{k}", tag=f"b_rows{k}", align_bytes=64)[:] for k in range(1)]
-        b_rows.append(picked_rest[:, PACK - 1, 0:P])
+        b_rows = [
+            pool.tile([P, P], F32, name="b_rows0", tag="b_rows0", align_bytes=64)[:],
+            picked_rest[:, PACK - 1, 0:P],
+        ]
         ident = pool.tile([P, P], F32, name="ident", tag="ident", align_bytes=64)
         bias = pool.tile([P, LATE_BIAS], F32, name="bias")
         late_bias = shared[:, HALF - (ROW_TILES - LATE_BIAS) : HALF]
@@ -96,8 +98,7 @@ def tile_list_hboth_silu_kernel(
 
         nc.vector.memset(w4_scales_early[:].bitcast(I32), 0)
         nc.vector.memset(windows[0][:], 0.0)
-        for rows in b_rows[1:]:
-            nc.gpsimd.memset(rows, 0.0)
+        nc.gpsimd.memset(b_rows[1], 0.0)
         nc.scalar.activation(b_rows[0], b_rows[1], SILU)
         make_identity(nc, ident[:])
         nc.gpsimd.memset(r8_scales_early[:].bitcast(I32), 0)
@@ -125,8 +126,8 @@ def tile_list_hboth_silu_kernel(
         def load_columns(tile, src, c0, c1):
             nc.sync.dma_start(tile[:, c0:c1], src[:, c0:c1])
 
-        nc.sync.dma_start(offs_t[:], offs)
         load_columns(wgt_t, wgt, *FRONT)
+        nc.sync.dma_start(offs_t[:], offs)
         for n in range(PLANES):
             nc.sync.dma_start(planes[n][:], x_rows[n // PACK, n % PACK])
             if n == 0:
@@ -141,9 +142,9 @@ def tile_list_hboth_silu_kernel(
         for r in range(SCALE_ROWS):
             load_scales(R8, r, 0, EARLY)
         load_r8(*CHUNKS[0])
-        load_weights(*CHUNKS[1])
         nc.sync.dma_start(offs2_t[:], offs2)
         load_columns(wgo_t, wgo, *FRONT)
+        load_weights(*CHUNKS[1])
         load_weights(*CHUNKS[2])
         load_columns(wgo_t, wgo, *REST)
         for r in range(SCALE_ROWS):
@@ -155,8 +156,7 @@ def tile_list_hboth_silu_kernel(
         for piece in range(len(BIAS_PIECES)):
             nc.tensor.transpose(banks[BIAS_BANK + piece][:, 0:P], b_rows[piece], ident[:])
         nc.scalar.copy(first_bias, banks[BIAS_BANK][:, 0:1])
-        for piece, (r0, r1) in enumerate(BIAS_PIECES[:1]):
-            nc.scalar.copy(bias[:, r0:r1], banks[BIAS_BANK + piece][:, 0 : r1 - r0])
+        nc.scalar.copy(bias[:], banks[BIAS_BANK][:, 0:LATE_BIAS])
 
         def picks(a, c0, c1):
             if a < LAST:

@@ -27,12 +27,14 @@ FRONT, REST, WHOLE = (0, HALF), (HALF, S), (0, S)
 W4, R8 = 0, 1
 SCALE_ROWS = 4
 SCALE_START = {W4: 0, R8: SCALE_ROWS}
+GROUP = 16
+BLOCK = 32
 WINDOWS = 3
 CHUNKS = ((0, P), (P, 2 * P), (2 * P, 3 * P), (3 * P, 5 * P), (5 * P, M))
 EARLY = 3 * P
 LATE_BIAS = ROW_TILES // 2
 BIAS_PIECES = ((0, LATE_BIAS), (LATE_BIAS, ROW_TILES))
-BIAS_BEHIND = (6, PLANES - 1)
+BIAS_BEHIND = (7, PLANES - 1)
 BIAS_BANK = 6
 SCALES_BEHIND = 7
 REST_STEP = S + 3 * S // 8
@@ -51,7 +53,10 @@ def tile_list_hboth_silu_kernel(
 
         offs_t = pool.tile([P, S // 16], U16, name="offs_t")
         offs2_t = pool.tile([P, S // 16], U16, name="offs2_t")
-        wgt_t = pool.tile([P, S], F32, name="wgt_t")
+        wgt_t = pool.tile([P, S], F32, name="wgt_t", align_bytes=64)
+        wgt_dealt = pool.tile([P, BLOCK], F32, name="wgt_dealt", align_bytes=64)
+        wgt_turned = pool.tile([P, BLOCK], F32, name="wgt_turned", align_bytes=64)
+        wgt_spread = pool.tile([P, S], F32, name="wgt_spread", align_bytes=64)
         wgo_t = pool.tile([P, S], F32, name="wgo_t")
         planes = [pool.tile([P, T], F32, name=f"plane{n}", align_bytes=64) for n in range(PLANES)]
         picked = [
@@ -126,12 +131,10 @@ def tile_list_hboth_silu_kernel(
         def load_columns(tile, src, c0, c1):
             nc.sync.dma_start(tile[:, c0:c1], src[:, c0:c1])
 
-        load_columns(wgt_t, wgt, *FRONT)
+        nc.sync.dma_start(wgt_dealt[:], wgt[0:P:GROUP, :].rearrange("g (m a) -> g m a", a=BLOCK))
         nc.sync.dma_start(offs_t[:], offs)
         for n in range(PLANES):
             nc.sync.dma_start(planes[n][:], x_rows[n // PACK, n % PACK])
-            if n == 0:
-                load_columns(wgt_t, wgt, *REST)
             if SCALES_BEHIND <= n < SCALES_BEHIND + SCALE_ROWS:
                 load_scales(W4, n - SCALES_BEHIND, 0, EARLY)
             if n in BIAS_BEHIND:
@@ -152,6 +155,17 @@ def tile_list_hboth_silu_kernel(
                 load_scales(kind, r, EARLY, M)
         load_weights(*CHUNKS[3])
         load_weights(*CHUNKS[4])
+
+        nc.vector.transpose(wgt_turned[:], wgt_dealt[:])
+        by_piece = wgt_turned[:].rearrange("p (e m) -> p m e", e=2)
+        for c0, c1 in (FRONT, REST):
+            m0, m1 = c0 // BLOCK, c1 // BLOCK
+            nc.vector.tensor_copy(
+                wgt_spread[:, c0:c1].rearrange("p (m e c) -> p m e c", e=2, c=GROUP),
+                by_piece[:, m0:m1, :].unsqueeze(3).to_broadcast([P, m1 - m0, 2, GROUP]),
+            )
+        for c0, c1 in (FRONT, REST):
+            nc.vector.transpose(wgt_t[:, c0:c1], wgt_spread[:, c0:c1])
 
         for piece in range(len(BIAS_PIECES)):
             nc.tensor.transpose(banks[BIAS_BANK + piece][:, 0:P], b_rows[piece], ident[:])
@@ -235,14 +249,13 @@ def tile_list_hboth_silu_kernel(
 
         first_of_last = LAST * PACK
         for n in range(first_of_last):
-            if n in (0, first_of_last - 1):
+            if n == 0:
                 gather(n, *FRONT)
                 gather(n, *REST)
             else:
                 gather(n, *WHOLE)
             if n % PACK == PACK - 1:
-                interleave(n // PACK, *FRONT)
-                interleave(n // PACK, *REST)
+                interleave(n // PACK, *WHOLE)
         codes[0] = pool.tile([P, S], U32, name="codes0", tag="b_rows0", align_bytes=64)
         quantize(0, *WHOLE)
 

@@ -34,7 +34,7 @@ CHUNKS = ((0, P), (P, 2 * P), (2 * P, 3 * P), (3 * P, 5 * P), (5 * P, M))
 EARLY = 3 * P
 LATE_BIAS = ROW_TILES // 2
 BIAS_PIECES = ((0, LATE_BIAS), (LATE_BIAS, ROW_TILES))
-BIAS_BEHIND = (7, PLANES - 1)
+BIAS_BEHIND = (6, PLANES - 1)
 BIAS_BANK = 6
 SCALES_BEHIND = 7
 REST_STEP = S + 3 * S // 8
@@ -56,9 +56,9 @@ def tile_list_hboth_silu_kernel(
         wgt_t = pool.tile([P, S], F32, name="wgt_t", align_bytes=64)
         wgt_dealt = pool.tile([P, BLOCK], F32, name="wgt_dealt", align_bytes=64)
         wgt_turned = pool.tile([P, BLOCK], F32, name="wgt_turned", align_bytes=64)
-        wgt_spread = pool.tile([P, S], F32, name="wgt_spread", align_bytes=64)
+        wgt_spread = pool.tile([P, S], F32, name="wgt_spread", tag="wgt_spread", align_bytes=64)
         wgo_t = pool.tile([P, S], F32, name="wgo_t")
-        planes = [pool.tile([P, T], F32, name=f"plane{n}", align_bytes=64) for n in range(PLANES)]
+        planes = [pool.tile([P, T], F32, name=f"plane{n}", tag=f"plane{n}", align_bytes=64) for n in range(PLANES)]
         picked = [
             pool.tile([P, PACK * S], F32, name=f"picked{a}")[:].rearrange("p (i s) -> p i s", i=PACK)
             for a in range(LAST)
@@ -76,15 +76,12 @@ def tile_list_hboth_silu_kernel(
         w4_t = {c0: pool.tile([P, PASSES, 2 * (c1 - c0)], U8, name=f"w4_{c0}", align_bytes=64) for c0, c1 in CHUNKS}
         r8_t = {c0: pool.tile([P, PASSES, 4 * (c1 - c0)], U8, name=f"r8_{c0}", align_bytes=64) for c0, c1 in CHUNKS}
         w4_scales_early = pool.tile([P, PASSES, EARLY], U8, name="w4_scales_early", align_bytes=64)
-        scales_late = pool.tile([P, PASSES, M - EARLY], U8, name="scales_late", align_bytes=64)
         r8_scales_early = pool.tile([P, PASSES, EARLY], U8, name="r8_scales_early", align_bytes=64)
         weight_scales = {
             (W4, 0): w4_scales_early,
             (R8, 0): r8_scales_early,
-            (W4, EARLY): scales_late,
-            (R8, EARLY): scales_late,
         }
-        windows = [pool.tile([P, T], F32, name=f"window{w}") for w in range(WINDOWS)]
+        windows = [pool.tile([P, T], F32, name="window0")]
         acts = [pool.tile([P, S], F32, name=f"act{r}") for r in range(ROW_TILES)]
         b_rows = [
             pool.tile([P, P], F32, name="b_rows0", tag="b_rows0", align_bytes=64)[:],
@@ -107,9 +104,6 @@ def tile_list_hboth_silu_kernel(
         nc.scalar.activation(b_rows[0], b_rows[1], SILU)
         make_identity(nc, ident[:])
         nc.gpsimd.memset(r8_scales_early[:].bitcast(I32), 0)
-        nc.gpsimd.memset(scales_late[:].bitcast(I32), 0)
-        for w in range(1, WINDOWS):
-            nc.gpsimd.memset(windows[w][:], 0.0)
 
         def load_scales(kind, r, c0, c1):
             src = (w4_scales, r8_scales)[kind]
@@ -150,12 +144,6 @@ def tile_list_hboth_silu_kernel(
         load_weights(*CHUNKS[1])
         load_weights(*CHUNKS[2])
         load_columns(wgo_t, wgo, *REST)
-        for r in range(SCALE_ROWS):
-            for kind in (W4, R8):
-                load_scales(kind, r, EARLY, M)
-        load_weights(*CHUNKS[3])
-        load_weights(*CHUNKS[4])
-
         nc.vector.transpose(wgt_turned[:], wgt_dealt[:])
         by_piece = wgt_turned[:].rearrange("p (e m) -> p m e", e=2)
         for c0, c1 in (FRONT, REST):
@@ -166,6 +154,16 @@ def tile_list_hboth_silu_kernel(
             )
         for c0, c1 in (FRONT, REST):
             nc.vector.transpose(wgt_t[:, c0:c1], wgt_spread[:, c0:c1])
+
+        scales_late = pool.tile([P, PASSES, M - EARLY], U8, name="scales_late", tag="wgt_spread", align_bytes=64)
+        nc.gpsimd.memset(scales_late[:].bitcast(I32), 0)
+        weight_scales[W4, EARLY] = scales_late
+        weight_scales[R8, EARLY] = scales_late
+        for r in range(SCALE_ROWS):
+            for kind in (W4, R8):
+                load_scales(kind, r, EARLY, M)
+        load_weights(*CHUNKS[3])
+        load_weights(*CHUNKS[4])
 
         for piece in range(len(BIAS_PIECES)):
             nc.tensor.transpose(banks[BIAS_BANK + piece][:, 0:P], b_rows[piece], ident[:])
@@ -249,13 +247,17 @@ def tile_list_hboth_silu_kernel(
 
         first_of_last = LAST * PACK
         for n in range(first_of_last):
-            if n == 0:
+            if n in (0, first_of_last - 1):
                 gather(n, *FRONT)
                 gather(n, *REST)
             else:
                 gather(n, *WHOLE)
             if n % PACK == PACK - 1:
-                interleave(n // PACK, *WHOLE)
+                interleave(n // PACK, *FRONT)
+                interleave(n // PACK, *REST)
+        for w, tag in ((1, "plane0"), (2, "plane1")):
+            windows.append(pool.tile([P, T], F32, name=f"window{w}", tag=tag, align_bytes=64))
+            nc.gpsimd.memset(windows[w][:], 0.0)
         codes[0] = pool.tile([P, S], U32, name="codes0", tag="b_rows0", align_bytes=64)
         quantize(0, *WHOLE)
 

@@ -126,9 +126,10 @@ def tile_list_hboth_silu_kernel(
             nc.sync.dma_start(tile[:, c0:c1], src[:, c0:c1])
 
         nc.sync.dma_start(wgt_dealt[:], wgt[0:P:GROUP, :].rearrange("g (m a) -> g m a", a=BLOCK))
-        nc.sync.dma_start(offs_t[:], offs)
         for n in range(PLANES):
             nc.sync.dma_start(planes[n][:], x_rows[n // PACK, n % PACK])
+            if n == 0:
+                nc.sync.dma_start(offs_t[:], offs)
             if SCALES_BEHIND <= n < SCALES_BEHIND + SCALE_ROWS:
                 load_scales(W4, n - SCALES_BEHIND, 0, EARLY)
             if n in BIAS_BEHIND:

from contextlib import ExitStack

import concourse.mybir as mybir
from concourse.masks import make_identity

F32 = mybir.dt.float32
BF16 = mybir.dt.bfloat16
I32 = mybir.dt.int32
U32 = mybir.dt.uint32
U16 = mybir.dt.uint16
U8 = mybir.dt.uint8
FP8X4 = mybir.dt.float8_e4m3fn_x4
FP4X4 = mybir.dt.float4_e2m1fn_x4
MULT = mybir.AluOpType.mult
SILU = mybir.ActivationFunctionType.Silu

K, M, T, S = 1536, 1024, 1024, 512
P = 128
PACK = 4
PASSES = K // (P * PACK)
LAST = PASSES - 1
PLANES = PASSES * PACK
ROW_TILES = M // P
HALF = S // 2
QUARTER = S // 4
FRONT, REST, WHOLE = (0, HALF), (HALF, S), (0, S)
W4, R8 = 0, 1
SCALE_ROWS = 4
SCALE_START = {W4: 0, R8: SCALE_ROWS}
GROUP = 16
BLOCK = 32
WINDOWS = 3
CHUNKS = ((0, P), (P, 2 * P), (2 * P, 3 * P), (3 * P, 5 * P), (5 * P, M))
EARLY = 3 * P
LATE_BIAS = ROW_TILES // 2
BIAS_PIECES = ((0, LATE_BIAS), (LATE_BIAS, ROW_TILES))
BIAS_BEHIND = (6, PLANES - 1)
BIAS_BANK = 6
SCALES_BEHIND = 7
REST_STEP = S + 3 * S // 8
BY_PASS = [(a, kind) for a in range(PASSES) for kind in (W4, R8)]
BY_LOAD = [(a, kind) for kind in (W4, R8) for a in range(LAST)] + [(LAST, W4), (LAST, R8)]
FLOPS = 2 * 2 * K * M * S


def tile_list_hboth_silu_kernel(
    tc, xT, w4_words, w4_scales, r8_words, r8_scales, wgt, b, wgo, offs, offs2, out
):
    nc = tc.nc
    with ExitStack() as ctx:
        pool = ctx.enter_context(tc.tile_pool(name="pool", bufs=1))
        psum = ctx.enter_context(tc.psum_pool(name="psum", bufs=1))

        offs_t = pool.tile([P, S // 16], U16, name="offs_t")
        offs2_t = pool.tile([P, S // 16], U16, name="offs2_t")
        wgt_t = pool.tile([P, S], F32, name="wgt_t", align_bytes=64)
        wgt_dealt = pool.tile([P, BLOCK], F32, name="wgt_dealt", align_bytes=64)
        wgt_turned = pool.tile([P, BLOCK], F32, name="wgt_turned", align_bytes=64)
        wgt_spread = pool.tile([P, S], F32, name="wgt_spread", tag="wgt_spread", align_bytes=64)
        wgo_t = pool.tile([P, S], F32, name="wgo_t")
        planes = [pool.tile([P, T], F32, name=f"plane{n}", tag=f"plane{n}", align_bytes=64) for n in range(PLANES)]
        picked = [
            pool.tile([P, PACK * S], F32, name=f"picked{a}")[:].rearrange("p (i s) -> p i s", i=PACK)
            for a in range(LAST)
        ]
        grouped = [pool.tile([P, S * PACK], BF16, name=f"grouped{a}", align_bytes=64) for a in range(LAST)]
        shared = pool.tile([P, HALF + PACK * REST_STEP], F32, name="shared")
        picked_front = shared[:, 0 : PACK * S].rearrange("p (i s) -> p i s", i=PACK)
        picked_rest = shared[:, HALF:].rearrange("p (i s) -> p i s", i=PACK)
        grouped_last = {
            part: pool.tile([P, HALF * PACK], BF16, name=f"grouped_last{part[0]}", align_bytes=64)
            for part in (FRONT, REST)
        }
        codes = {LAST: pool.tile([P, S], U32, name="codes_last", align_bytes=64)}
        scales = [pool.tile([P, S], U8, name=f"scales{a}", align_bytes=64) for a in range(PASSES)]
        w4_t = {c0: pool.tile([P, PASSES, 2 * (c1 - c0)], U8, name=f"w4_{c0}", align_bytes=64) for c0, c1 in CHUNKS}
        r8_t = {c0: pool.tile([P, PASSES, 4 * (c1 - c0)], U8, name=f"r8_{c0}", align_bytes=64) for c0, c1 in CHUNKS}
        w4_scales_early = pool.tile([P, PASSES, EARLY], U8, name="w4_scales_early", align_bytes=64)
        r8_scales_early = pool.tile([P, PASSES, EARLY], U8, name="r8_scales_early", align_bytes=64)
        weight_scales = {
            (W4, 0): w4_scales_early,
            (R8, 0): r8_scales_early,
        }
        windows = [pool.tile([P, T], F32, name="window0")]
        acts = [pool.tile([P, S], F32, name=f"act{r}") for r in range(ROW_TILES)]
        b_rows = [
            pool.tile([P, P], F32, name="b_rows0", tag="b_rows0", align_bytes=64)[:],
            picked_rest[:, PACK - 1, 0:P],
        ]
        ident = pool.tile([P, P], F32, name="ident", tag="ident", align_bytes=64)
        bias = pool.tile([P, LATE_BIAS], F32, name="bias")
        late_bias = shared[:, HALF - (ROW_TILES - LATE_BIAS) : HALF]
        first_bias = grouped_last[REST][:, 0:2].bitcast(F32)
        banks = [psum.tile([P, S], F32, name=f"bank{k}") for k in range(8)]

        x_rows = xT.rearrange("(a p i) t -> a i p t", p=P, i=PACK)
        b_by_tile = b.rearrange("(r p) -> r p", p=P)
        w4_src = w4_words.bitcast(I32).rearrange("a p c -> p a c")
        r8_src = r8_words.rearrange("a p n i -> a p (n i)").bitcast(I32).rearrange("a p c -> p a c")

        nc.vector.memset(w4_scales_early[:].bitcast(I32), 0)
        nc.vector.memset(windows[0][:], 0.0)
        nc.gpsimd.memset(b_rows[1], 0.0)
        nc.scalar.activation(b_rows[0], b_rows[1], SILU)
        make_identity(nc, ident[:])
        nc.gpsimd.memset(r8_scales_early[:].bitcast(I32), 0)

        def load_scales(kind, r, c0, c1):
            src = (w4_scales, r8_scales)[kind]
            nc.sync.dma_start(
                weight_scales[kind, c0][SCALE_START[kind] + r : P : 32].bitcast(I32),
                src[:, :, c0:c1].bitcast(I32).rearrange("a (q r) n -> r q a n", r=SCALE_ROWS)[r],
            )

        def load_w4(c0, c1):
            nc.sync.dma_start(w4_t[c0][:].bitcast(I32), w4_src[:, :, c0 // 2 : c1 // 2])

        def load_r8(c0, c1):
            nc.sync.dma_start(r8_t[c0][:].bitcast(I32), r8_src[:, :, c0:c1])

        def load_weights(c0, c1):
            load_w4(c0, c1)
            load_r8(c0, c1)

        def load_columns(tile, src, c0, c1):
            nc.sync.dma_start(tile[:, c0:c1], src[:, c0:c1])

        nc.sync.dma_start(wgt_dealt[:], wgt[0:P:GROUP, :].rearrange("g (m a) -> g m a", a=BLOCK))
        for n in range(PLANES):
            nc.sync.dma_start(planes[n][:], x_rows[n // PACK, n % PACK])
            if n == 0:
                nc.sync.dma_start(offs_t[:], offs)
            if SCALES_BEHIND <= n < SCALES_BEHIND + SCALE_ROWS:
                load_scales(W4, n - SCALES_BEHIND, 0, EARLY)
            if n in BIAS_BEHIND:
                piece = BIAS_BEHIND.index(n)
                r0, r1 = BIAS_PIECES[piece]
                nc.sync.dma_start(b_rows[piece][0 : r1 - r0, :], b_by_tile[r0:r1])
        load_w4(*CHUNKS[0])
        for r in range(SCALE_ROWS):
            load_scales(R8, r, 0, EARLY)
        load_r8(*CHUNKS[0])
        nc.sync.dma_start(offs2_t[:], offs2)
        load_columns(wgo_t, wgo, *FRONT)
        load_weights(*CHUNKS[1])
        load_weights(*CHUNKS[2])
        load_columns(wgo_t, wgo, *REST)
        nc.vector.transpose(wgt_turned[:], wgt_dealt[:])
        by_piece = wgt_turned[:].rearrange("p (e m) -> p m e", e=2)
        for c0, c1 in (FRONT, REST):
            m0, m1 = c0 // BLOCK, c1 // BLOCK
            nc.vector.tensor_copy(
                wgt_spread[:, c0:c1].rearrange("p (m e c) -> p m e c", e=2, c=GROUP),
                by_piece[:, m0:m1, :].unsqueeze(3).to_broadcast([P, m1 - m0, 2, GROUP]),
            )
        for c0, c1 in (FRONT, REST):
            nc.vector.transpose(wgt_t[:, c0:c1], wgt_spread[:, c0:c1])

        scales_late = pool.tile([P, PASSES, M - EARLY], U8, name="scales_late", tag="wgt_spread", align_bytes=64)
        nc.gpsimd.memset(scales_late[:].bitcast(I32), 0)
        weight_scales[W4, EARLY] = scales_late
        weight_scales[R8, EARLY] = scales_late
        for r in range(SCALE_ROWS):
            for kind in (W4, R8):
                load_scales(kind, r, EARLY, M)
        load_weights(*CHUNKS[3])
        load_weights(*CHUNKS[4])

        for piece in range(len(BIAS_PIECES)):
            nc.tensor.transpose(banks[BIAS_BANK + piece][:, 0:P], b_rows[piece], ident[:])
        nc.scalar.copy(first_bias, banks[BIAS_BANK][:, 0:1])
        nc.scalar.copy(bias[:], banks[BIAS_BANK][:, 0:LATE_BIAS])

        def picks(a, c0, c1):
            if a < LAST:
                return picked[a][:, :, c0:c1]
            if c0 < HALF:
                return picked_front[:, :, c0:c1]
            return picked_rest[:, :, c0 - HALF : c1 - HALF]

        def rounded(a, c0, c1):
            if a < LAST:
                return grouped[a][:, PACK * c0 : PACK * c1]
            part = FRONT if c1 <= HALF else REST
            return grouped_last[part][:, PACK * (c0 - part[0]) : PACK * (c1 - part[0])]

        def gather(n, c0, c1):
            nc.vector.tensor_tensor(
                picks(n // PACK, c0, c1)[:, n % PACK, :],
                planes[n][:].indirect(offs_t[:, c0 // 16 : c1 // 16]),
                wgt_t[:, c0:c1],
                MULT,
            )

        def interleave(a, c0, c1):
            nc.scalar.copy(
                rounded(a, c0, c1).rearrange("p (c j i) -> p c i j", j=4, i=PACK),
                picks(a, c0, c1).rearrange("p i (c j) -> p c i j", j=4),
            )

        def quantize(a, c0, c1):
            nc.vector.quantize_mx(
                out=codes[a][:, c0:c1].bitcast(FP8X4), scales=scales[a][:, c0:c1], in_=rounded(a, c0, c1)
            )

        def multiply(r, a, kind, c0, c1, bank):
            chunk = max(start for start, end in CHUNKS if start <= P * r)
            n0 = P * r - chunk
            base = 0 if P * r < EARLY else EARLY
            lhsT_scale = weight_scales[kind, base][SCALE_START[kind] : P, a, P * r - base : P * (r + 1) - base]
            if kind == W4:
                lhsT = w4_t[chunk][:, a, 2 * n0 : 2 * (n0 + P)].bitcast(FP4X4)
                width = S if c1 - c0 == S else QUARTER
            else:
                lhsT = r8_t[chunk][:, a, 4 * n0 : 4 * (n0 + P)].bitcast(FP8X4)
                width = c1 - c0
            for c in range(c0, c1, width):
                nc.tensor.matmul_mx(
                    out=bank[:, c - c0 : c - c0 + width],
                    lhsT=lhsT,
                    lhsT_scale=lhsT_scale,
                    rhs=codes[a][:, c : c + width].bitcast(FP8X4),
                    rhs_scale=scales[a][:, c : c + width],
                    start=((a, kind, c) == (0, W4, c0)),
                    stop=((a, kind) == (LAST, R8)),
                )

        def multiply_group(r, c0, c1, bank, order):
            for a, kind in order:
                multiply(r, a, kind, c0, c1, bank)

        def activate(r, c0, c1, bank):
            if (r, c0) == (0, 0):
                column = first_bias
            elif r < LATE_BIAS:
                column = bias[:, r : r + 1]
            else:
                column = late_bias[:, r - LATE_BIAS : r - LATE_BIAS + 1]
            nc.scalar.activation(acts[r][:, c0:c1], bank[:, 0 : c1 - c0], SILU, bias=column)

        def scatter(r, c0, c1):
            window = windows[r % WINDOWS]
            nc.vector.tensor_tensor(
                window[:].indirect(offs2_t[:, c0 // 16 : c1 // 16]), acts[r][:, c0:c1], wgo_t[:, c0:c1], MULT
            )
            if c1 == S:
                nc.sync.dma_start(out[P * r : P * (r + 1), :], window[:])

        first_of_last = LAST * PACK
        for n in range(first_of_last):
            if n in (0, first_of_last - 1):
                gather(n, *FRONT)
                gather(n, *REST)
            else:
                gather(n, *WHOLE)
            if n % PACK == PACK - 1:
                interleave(n // PACK, *FRONT)
                interleave(n // PACK, *REST)
        for w, tag in ((1, "plane0"), (2, "plane1")):
            windows.append(pool.tile([P, T], F32, name=f"window{w}", tag=tag, align_bytes=64))
            nc.gpsimd.memset(windows[w][:], 0.0)
        codes[0] = pool.tile([P, S], U32, name="codes0", tag="b_rows0", align_bytes=64)
        quantize(0, *WHOLE)

        gather(first_of_last, *WHOLE)
        for n in range(first_of_last + 1, PLANES - 1):
            gather(n, *FRONT)
        for c0 in (0, QUARTER):
            gather(PLANES - 1, c0, c0 + QUARTER)
            interleave(LAST, c0, c0 + QUARTER)
        nc.scalar.copy(late_bias, banks[BIAS_BANK + 1][:, 0 : ROW_TILES - LATE_BIAS])
        codes[1] = pool.tile([P, S], U32, name="codes1", tag="ident", align_bytes=64)
        quantize(1, *WHOLE)
        gather(PLANES - 1, *REST)
        quantize(LAST, *FRONT)
        multiply_group(0, *FRONT, banks[0], BY_PASS)
        for n in range(first_of_last + 1, PLANES - 1):
            gather(n, *REST)
        activate(0, *FRONT, banks[0])
        interleave(LAST, *REST)

        scatter(0, *FRONT)
        multiply_group(1, *FRONT, banks[1], BY_LOAD)
        activate(1, *FRONT, banks[1])
        multiply_group(0, *REST, banks[2], BY_PASS[:-2])
        multiply_group(1, *REST, banks[3], BY_LOAD[:-2])
        quantize(LAST, *REST)
        multiply_group(0, *REST, banks[2], BY_PASS[-2:])
        activate(0, *REST, banks[2])
        scatter(1, *FRONT)
        scatter(0, *REST)
        multiply_group(1, *REST, banks[3], BY_LOAD[-2:])
        activate(1, *REST, banks[3])
        scatter(1, *REST)

        for r in range(2, ROW_TILES):
            bank = banks[(r + 2) % len(banks)]
            multiply_group(r, *WHOLE, bank, BY_LOAD)
            activate(r, *WHOLE, bank)
            scatter(r, *WHOLE)
